import numpy as np, ml_dtypes
CORES = [13,21,141,149]
N = 4
BF = ml_dtypes.bfloat16
def gentries(a):
    return np.ascontiguousarray(a.reshape(8, 16, -1).transpose(0, 2, 1)).reshape(8, -1)
def gtable(e):
    e = np.asarray(e); return np.ascontiguousarray(e.reshape(8, -1, 16).transpose(0, 2, 1)).reshape(128, -1).astype(np.int32)
W, K, L, T = 2048, 768, 2, 2
TOP, NEG, EMPTY = 255, 9, 16
def parts(rng):
    j = rng.integers(0, W, (N, 8, 16, W), dtype=np.int32)
    x = rng.integers(0, 16, (N, 8, N, L, K)); x = np.where(rng.random(x.shape) < 0.125, EMPTY, x)
    return j, x, rng.integers(0, 16, (N, 8, K)), rng.integers(0, W, (N, 8, T, K))
def coef(rng, drift):
    c = drift + 50.0 * rng.standard_normal((N, 8, 1, W), dtype=np.float32) + 40.0 * rng.standard_normal((N, 8, 16, W), dtype=np.float32)
    return np.minimum(np.maximum(np.rint(c), -128), 127)
def pack(j, c, x, y, a):
    return {"jm": np.ascontiguousarray(j.reshape(N, 128, W)).astype(np.int32), "cf": (np.ascontiguousarray(c.reshape(N, 128, W)).astype(np.float32) + 0.0).astype(BF),
            "lt": np.ascontiguousarray(x.reshape(N, 8, N * L * K)).astype(np.float32).astype(BF), "y0": np.ascontiguousarray(y).astype(np.float32).astype(BF),
            "st": np.stack([gtable(q.reshape(8, T * K)) for q in a])}
def setup_inputs(rng):
    j, x, y, a = parts(rng)
    return pack(j, coef(rng, rng.choice(np.array([5.0, 15.0, 30.0, 45.0]), (N, 8, 1, 1))), x, y, a)
def setup_inputs_ties(rng):
    j, x, y, a = parts(rng); n = rng.choice(np.array([4, 6, 7, 8, 9]), (N, 8, 1, W))
    o = np.argsort(rng.random((N, 8, 16, W)), axis=2); c = np.where(o < n, -1, (rng.random(o.shape) < 0.8).astype(np.int64))
    p = rng.permutation(16)[:, None]
    c[:, 0] = np.where(p < 8, -1, 1); c[:, 1] = np.where(p < 9, -1, 1); c[:, 2] = np.where(p < 8, -1, 0)
    return pack(j, c, x, y, a)
def setup_inputs_clip(rng):
    j, x, y, a = parts(rng); s = np.where(rng.random((N, 8, 1, W)) < 0.75, 1, -1)
    c = s * rng.integers(100, 128, (N, 8, 16, W)); c = np.where(rng.random(c.shape) < 0.1, -c, c)
    c[:, 1::2, :5] = -np.abs(c[:, 1::2, :5]) - 1
    r = int(rng.integers(0, N)); x[:, 6, r] = rng.integers(0, 16, (N, L, K)); e = 127 // L
    for d in range(N):
        q = (r + d) % N; c[q, 6] = 1; c[q, 6, 1:8] = -1
        c[q, 6, 8] = -1 if d == 3 else 0
        c[q, 6, 0] = (-128, e, e, 255 - 2 * L * e)[d] if d < 4 else 0
    return pack(j, c, x, y, a)
def setup_inputs_gaps(rng):
    j, x, y, a = parts(rng); x = np.where(rng.random(x.shape) < 0.5, EMPTY, x)
    x[:, 0] = EMPTY; x[:, 1:4] = rng.integers(0, 16, (N, 3, N, L, K))
    for q in range(N):
        for s in range(N):
            if q != s: x[q, 2, s] = EMPTY
            if q != (s - 1) % N: x[q, 3, s] = EMPTY
    c = coef(rng, 20.0); r = int(rng.integers(0, N))
    c[r, 0] = -rng.integers(1, 129, (16, W)); c[r, 1] = -128; c[r, 1, 8:] += (rng.random(W) < 0.5).astype(np.float32)
    x[r, 1, r, 1:] = EMPTY
    return pack(j, c, x, y, a)
def setup_inputs_alike(rng):
    j, x, y, a = parts(rng)
    j[:, ::2] = rng.choice(np.array([0, W - 1, W // 2, 5], np.int32), (N, 4, 16, W)); j[:, 1] = np.arange(W)
    j[:, 6] = rng.integers(0, W, (N, 1, 1))
    x[:, 3] = rng.integers(0, 16, (N, 1, 1, 1)); y[:, 3] = rng.integers(0, 16, (N, 1))
    a[:, 2] = rng.integers(0, W, (N, 1, 1)); a[:, 5] = rng.choice(np.array([0, W - 1]), (N, T, K))
    c = coef(rng, 25.0); r = int(rng.integers(0, N)); c[r] = np.minimum(np.abs(c[r]), 127)
    return pack(j, c, x, y, a)
def setup_inputs_spread(rng):
    j, x, y, a = parts(rng)
    j = np.minimum((W * rng.random(j.shape) ** 3).astype(np.int64), W - 1); a = np.minimum((W * rng.random(a.shape) ** 3).astype(np.int64), W - 1)
    c = np.exp2(8.0 * rng.random((N, 8, 1, W))) * (0.5 * rng.standard_normal((N, 8, 16, W)) + 0.25)
    x = np.minimum((17 * rng.random(x.shape) ** 2).astype(np.int64), EMPTY); y = np.minimum((16 * rng.random(y.shape) ** 2).astype(np.int64), 15)
    return pack(j, np.minimum(np.maximum(np.rint(c), -128), 127), x, y, a)
def check_inputs(d):
    bad = []
    for k, lo, hi in (("jm", 0, W - 1), ("cf", -128, 127), ("lt", 0, 16), ("y0", 0, 15), ("st", 0, W - 1)):
        a = np.asarray(d[k]).astype(np.float32)
        if not (np.all(a == np.floor(a)) and np.min(a) >= lo and np.max(a) <= hi): bad.append("range of " + k)
        if np.any(np.signbit(a) & (a == 0)): bad.append("-0.0 in " + k)
    return bad
def reference(jm, cf, lt, y0, st):
    J = jm.astype(np.int64).reshape(N, 8, 16, W); C = cf.astype(np.float32).astype(np.int64).reshape(N, 8, 16, W)
    x = lt.astype(np.float32).astype(np.int64).reshape(N, 8, N, L, K); y = y0.astype(np.float32).astype(np.int64)
    start = np.stack([gentries(a) for a in st]).astype(np.int64).reshape(N, 8, T, K)
    new = np.full((N, 8, T, K), EMPTY, np.int64); v = np.zeros((N, 8, 16, K), np.int64); g = np.arange(8)[:, None]
    for t in range(T):
        for s in range(N):
            b = J[s][g, y[s], start[s, :, t]]; u = np.take_along_axis(C[s], b[:, None, :], 2)
            live = np.ones((8, K), bool)
            for d in range(N):
                q = (s + d) % N
                slots = [new[s, :, i] for i in range(t - 1, -1, -1)] if d == 0 else []
                for z in slots + [x[q, :, s, l] for l in range(L)]:
                    go = live & (z < EMPTY)
                    b = np.where(go, J[q][g, np.minimum(z, 15), b], b)
                    w = np.minimum(np.maximum(u + np.take_along_axis(C[q], b[:, None, :], 2), -TOP), TOP)
                    u = np.where(go[:, None, :], w, u)
                    hit = go & (np.add.reduce((u < 0).astype(np.int64), axis=1) >= NEG)
                    z[hit] = EMPTY; live = live & ~hit
            new[s, :, t] = np.where(live, y[s], EMPTY)
            y[s] = np.argmax(u, axis=1)
            v[s] = u
    return {"yl": x.reshape(N, 8, N * L * K).astype(np.float32).astype(BF), "yi": new.reshape(N, 8, T * K).astype(np.float32).astype(BF), "yv": v.reshape(N, 128, K).astype(np.float32).astype(BF)}

@@ -1,0 +1,608 @@
+from concourse.bass import DstId, RemoteDMATransfer
+from concourse.mybir import AluOpType as A, ActivationFunctionType as F
+
+OUTW = 4 * 3840 + 2304
+SCRATCH = {}
+for _ty, _s in (
+        ("bfloat16", "C0 2064 C1 2064 C2 2064 C3 2064 OHY 768 SG0 768 SG1 768 SG2 768 SG3 768 D0A 3840 D0B 3840 D1 3840 D0S 2304 D1S 2304 "
+         "VF 768 VN 768 LTA 384 LTS 384 LF 384 LT1 384 LZ 384 LI1 96 LI2 96 LI3 96 Y0W 64 YI0 64 YI1 64 KC 48 YT 128 ET 32 IDB 128 ID16 128 "
+         "SBB 144 SBX 144 EBA 768 EBB 768 EBC 768 IR 384 ONE 128 PAT 384 OUT %d " % OUTW + " ".join("OH%d 768" % k for k in range(9))),
+        ("int32", "J0 2056 J1 2056 J2 2056 J3 2056 STI 96 KI 48 KB 48 PI 8 PJ 8"),
+        ("float16", "MJ0 768 MJ1 768 STF 768 BE0 48 BE1 48 Z0 432 Z02 432 Z1 432 Z12 432 ZD 432 IDF 128 SBF 144"),
+        ("uint16", "STU 96 OFS 96 OFJ 48 OC0 48 OC1 48 LU 384 Y0U 48 SEL 48"),
+        ("float32", "KM 768 IOT 2048 TC0 48 TC1 48 Y1W 48 ZZ0 432 ZZ1 432 M0 48 M1 48 EE 48 DL 48 DM 48 T1 48 T2 48 PC 8 P15 8 V8 8 V8A 8 V8B 8 "
+         "XR 32 JR 48 JW 48 B5 48 DD 48 IV 128"),
+        ("psum", "XA 512 XB 512 KA 512 KBK 512 KEY 1024 YB 1024")):
+    _p = _s.split()
+    for _n, _w in zip(_p[::2], _p[1::2]):
+        SCRATCH[_n] = ("psum", [128, int(_w)], "float32") if _ty == "psum" else ("sbuf", [128, int(_w)], _ty)
+
+SEMAPHORES = "qv qs qp qg dJA dJB dC dSt dLo dLr dO lo rJ rC rL rF".split()
+SEMAPHORES += ["%s%d" % (a, d) for a in ("aJ", "aC", "aL", "aF") for d in (1, 2, 3)]
+
+WORLD = 256
+BIG = 40000.0
+QK = [BIG - (3840 * (k // 2) + 2 + 2 * (k % 2)) for k in range(8)] + [1.0]
+
+
+def routes(topo, cores, r):
+    c, n = cores[r], len(cores)
+    x1, x3 = cores[(r - 1) % n], cores[(r - 3) % n]
+    own = [e for e in topo.cores_of(c) if e != c and topo.may_write(e, x1)]
+    same = [e for e in own if topo.die(e) == topo.die(c)]
+    oth = [e for e in own if topo.die(e) != topo.die(c)]
+    relays = [same[0], oth[0], same[1], oth[1]]
+    far = [e for e in range(WORLD) if topo.mates(e, x3) and topo.may_write(e, x3)]
+    pick = []
+    for e in relays:
+        pick.append([y for y in far if topo.die(y) == topo.die(e) and y not in pick][0])
+    return relays, pick
+
+
+def hand_on(g, core, T, topo):
+    cores, n = T.cores, len(T.cores)
+    lo = [0]
+
+    def send(dst, out, in_, sem):
+        rid, pid = topo.addr(dst, core)
+        g.remote_dma(out, in_, T.sem[sem], T.sem.lo, pid, rid, topo.mask(core, dst))
+        lo[0] += len(topo.engines(core, dst))
+
+    for r in range(n):
+        relays, far = routes(topo, cores, r)
+        if core in relays:
+            i = relays.index(core)
+            x = [cores[(r - d) % n] for d in range(n)]
+            cs = slice(512 * i, 512 * i + 512)
+            g.wait_ge(T.sem.rJ, 8)
+            send(x[1], T.J1[:, cs], T.J0[:, cs], "aJ1")
+            if i in (0, 2):
+                d = 1 if i == 0 else 3
+                g.wait_ge(T.sem.rL, 4)
+                send(x[d], T.LTA[:, 96 * d:96 * d + 96], T.LI1[:], "aL%d" % d)
+            g.wait_ge(T.sem.rC, 4)
+            send(x[1], T.C1[:, cs], T.C0[:, cs], "aC1")
+            send(x[2], T.J2[:, cs], T.J0[:, cs], "aJ2")
+            send(far[i], T.J0[:, cs], T.J0[:, cs], "rJ")
+            send(x[2], T.C2[:, cs], T.C0[:, cs], "aC2")
+            send(far[i], T.C0[:, cs], T.C0[:, cs], "rC")
+            if i in (0, 2):
+                d = 3 if i == 0 else 1
+                g.wait_ge(T.sem.rF, 8)
+                send(cores[(r + d) % n], T["LI%d" % d][:], T.LI2[:], "aF%d" % d)
+        if core in far:
+            i = far.index(core)
+            x3 = cores[(r - 3) % n]
+            cs = slice(512 * i, 512 * i + 512)
+            k = len(topo.engines(relays[i], core))
+            g.wait_ge(T.sem.rJ, k)
+            send(x3, T.J3[:, cs], T.J0[:, cs], "aJ3")
+            g.wait_ge(T.sem.rC, k)
+            send(x3, T.C3[:, cs], T.C0[:, cs], "aC3")
+    if lo[0]:
+        g.wait_ge(T.sem.lo, lo[0])
+
+
+def rank_program(g, core, T, topo):
+    rank = T.rank_of(core)
+    if rank is None:
+        hand_on(g, core, T, topo)
+        return
+    cores, n = T.cores, len(T.cores)
+    relays, far = routes(topo, cores, rank)
+    Q = {"v": g.vector, "s": g.scalar, "p": g.tensor, "g": g, "y": g.sync}
+    SEM = {"v": "qv", "s": "qs", "p": "qp", "g": "qg"}
+    cnt = {q: 0 for q in SEM}
+    clock = {q: {} for q in Q}
+    lastw, readers = {}, {}
+
+    def need(q, toks):
+        best = {}
+        for t in toks:
+            if t and clock[q].get(t[0], 0) < t[1] and (t[0] not in best or best[t[0]][1] < t[1]):
+                best[t[0]] = t
+        for t in sorted(best.values(), key=lambda t: -len(t[2])):
+            if clock[q].get(t[0], 0) >= t[1]:
+                continue
+            Q[q].wait_ge(T.sem[t[0]], t[1])
+            for s, v in t[2].items():
+                if clock[q].get(s, 0) < v:
+                    clock[q][s] = v
+
+    def deps(q, reads, writes):
+        out = [lastw.get(r) for r in reads]
+        for w in writes:
+            t = lastw.get(w)
+            if t and not (q == "p" and t[0] == "qp"):
+                out.append(t)
+            out += readers.get(w, [])
+        return out
+
+    def done(tok, reads, writes):
+        for r in reads:
+            readers.setdefault(r, []).append(tok)
+        for w in writes:
+            lastw[w] = tok
+            readers[w] = []
+
+    def op(q, call, reads, writes):
+        need(q, deps(q, reads, writes))
+        cnt[q] += 1
+        call().then_inc(T.sem[SEM[q]], 1)
+        c = dict(clock[q])
+        c[SEM[q]] = cnt[q]
+        done((SEM[q], cnt[q], c), reads, writes)
+
+    def pe(items, writes):
+        allr = []
+        for i, (o, l, r, rd) in enumerate(items):
+            need("p", deps("p", rd, writes if i == 0 else []))
+            allr += rd
+            ins = g.tensor.matmul(o, l, r, i == 0, i == len(items) - 1)
+        cnt["p"] += 1
+        ins.then_inc(T.sem.qp, 1)
+        c = dict(clock["p"])
+        c["qp"] = cnt["p"]
+        done(("qp", cnt["p"], c), allr, writes)
+
+    def dma(q, out, in_, sem, total, reads, writes):
+        need(q, [t for t in deps(q, reads, writes) if t and t[0] != sem])
+        Q[q].dma_start(out, in_).then_inc(T.sem[sem], 16)
+        c = dict(clock[q])
+        c[sem] = total
+        done((sem, total, c), reads, writes)
+
+    def ts(out, in0, a, b, o0, o1, reads, writes):
+        if o1 is None:
+            op("v", lambda: g.vector.tensor_scalar(out, in0, a, None, o0), reads, writes)
+        else:
+            op("v", lambda: g.vector.tensor_scalar(out, in0, a, b, o0, o1), reads, writes)
+
+    def tt(out, a, b, o, reads, writes):
+        op("v", lambda: g.vector.tensor_tensor(out, a, b, o), reads, writes)
+
+    def cp(out, a, reads, writes):
+        op("v", lambda: g.vector.tensor_copy(out, a), reads, writes)
+
+    def fill(ap, val, writes):
+        op("v", lambda: g.vector.memset(ap, val), [], writes)
+
+    def act(out, in_, func, reads, writes, bias=0.0, scale=1.0):
+        op("s", lambda: g.scalar.activation(out, in_, func, bias=bias, scale=scale), reads, writes)
+
+    def iota(out, pattern, base, ch, writes):
+        op("g", lambda: g.iota(out, pattern, base, ch, allow_small_or_imprecise_dtypes=True), [], writes)
+
+    def blk(name, k, m=1):
+        return T[name][:, 48 * k:48 * (k + m)]
+
+    def ks(name, r):
+        return ["%s%d" % (name, k) for k in r]
+
+    dma("y", T.STI[:], T.st[:], "dSt", 16, [], ["STI"])
+    dma("s", T.J0[:, 0:1024], T.jm[:, 0:1024], "dJA", 16, [], ["J0a"])
+    for l in range(2):
+        a = (rank * 2 + l) * 768
+        dma("y", T.LTA[:, 48 * l:48 * l + 48], T.lt[:, a:a + 768], "dLo", 48, [], ["LTA0"])
+    dma("y", T.Y0W[:, 0:48], T.y0[:], "dLo", 48, [], ["Y0W"])
+    dma("s", T.J0[:, 1024:2048], T.jm[:, 1024:2048], "dJB", 16, [], ["J0b"])
+    dma("s", T.C0[:, 0:2048], T.cf[:], "dC", 16, [], ["C0"])
+    for d in range(1, n):
+        s = (rank - d) % n
+        for l in range(2):
+            a = (s * 2 + l) * 768
+            b = 96 * s + 48 * l
+            dma("y", T.LTS[:, b:b + 48], T.lt[:, a:a + 768], "dLr", 96, [], ["LTS"])
+    for d in range(1, n):
+        for a, w, k in (("aJ", "J", 32), ("aC", "C", 32), ("aL", "LTA", 8 if d != 2 else 2)):
+            nm = "%s%d" % (a, d)
+            lastw["%s%d" % (w, d)] = (nm, k, {nm: k})
+
+    iota(T.PI[:, 0:1], [[0, 1]], 0, 1, ["PI"])
+    iota(T.V8[:], [[-16, 8]], 0, 1, ["V8"])
+    iota(T.IOT[:, 0:512], [[1, 512]], 0, 0, ["IOT0"])
+    iota(T.XR[:], [[1, 32]], 0, 0, ["XR"])
+    iota(T.JR[:], [[16, 48]], 0, 0, ["JR"])
+    iota(T.IV[:], [[-1, 128]], 0, 1, ["IV"])
+
+    for d in range(4):
+        fill(T["J%d" % d][:, 2048:2056], 0, ["Jz%d" % d])
+        fill(T["C%d" % d][:, 2048:2064], 0.0, ["Cz%d" % d])
+    fill(T.SBB[:], 0.0, ["SBB"])
+    fill(T.ONE[:], 1.0, ["ONE"])
+    ts(T.PJ[:, 0:1], T.PI[:, 0:1], 15, None, A.bitwise_and, None, ["PI"], ["PJ"])
+    ts(T.V8A[:], T.V8[:], -0.5, None, A.is_gt, None, ["V8"], ["V8A"])
+    ts(T.V8B[:], T.V8[:], 15.5, None, A.is_lt, None, ["V8"], ["V8B"])
+    cp(T.PC[:, 0:1], T.PJ[:, 0:1], ["PJ"], ["PC"])
+    tt(T.SBB[:, 15:143:16], T.V8A[:], T.V8B[:], A.mult, ["V8A", "V8B"], ["SBB"])
+    for k in (1, 2, 3):
+        ts(T.IOT[:, 512 * k:512 * k + 512], T.IOT[:, 0:512], 512.0 * k, None, A.add, None, ["IOT0"], ["IOT%d" % k])
+    cp(T.SBF[:], T.SBB[:], ["SBB"], ["SBF"])
+    ts(T.ET[:], T.XR[:], T.PC[:, 0:1], None, A.is_equal, None, ["XR", "PC"], ["ET"])
+    ts(T.IDF[:], T.IV[:], 0.0, None, A.is_equal, None, ["IV"], ["IDF"])
+
+    def sels(o, buf, rd, sb="SBF", contiguous=False):
+        src = T[buf]
+        out = []
+        for h in range(16):
+            v = src[:, 48 * h:48 * h + 48] if contiguous else src[:, h:768:16]
+            out.append((o, T[sb][:, 15 - h:143 - h], v, [rd, sb]))
+        return out
+
+    def starts(t):
+        op("v", lambda: g.vector.tensor_copy(T.STF[:], T.IOT[:, 0:2048].indirect(blk("STU", t))), ks("IOT", range(4)) + ["STU"], ["STF"])
+        pe(sels(T.KEY[:, 512 * t:512 * t + 48], "STF", "STF", contiguous=True), ["KEY%d" % t])
+
+    def starts2(t):
+        ts(blk("OFS", t), T.KEY[:, 512 * t:512 * t + 48], 0.0625, None, A.mult, None, ["KEY%d" % t], ["OFS%d" % t])
+
+    def letters(d):
+        src, k = T.LTA[:, 96 * d:96 * d + 96], 2 * d + 1
+        L = "LTA%d" % d
+        cp(T.LU[:, 96 * d:96 * d + 96], src, [L], ["LU%d" % d])
+        ts(blk("Z0", k, 2), src, 15.5, 4096.0, A.is_gt, A.mult, [L], ks("Z0_", (k, k + 1)))
+        ts(blk("Z02", k, 2), src, 15.5, 8192.0, A.is_gt, A.mult, [L], ks("Z02_", (k, k + 1)))
+        if d == 0:
+            tt(blk("ZZ0", 1), blk("Z02", 1), blk("Z0", 2), A.subtract, ["Z02_1", "Z0_2"], ["ZZ0_1"])
+        else:
+            e = 2 * d
+            tt(blk("ZZ0", e, 2), blk("Z02", e, 2), blk("Z0", e + 1, 2), A.subtract,
+               ks("Z02_", (e, e + 1)) + ks("Z0_", (e + 1, e + 2)), ks("ZZ0_", (e, e + 1)))
+        if d == 3:
+            cp(blk("ZZ0", 8), blk("Z02", 8), ["Z02_8"], ["ZZ0_8"])
+
+    def onehot(k):
+        off = T.Y0U[:] if k == 0 else T.LU[:, 48 * (k - 1):48 * k]
+        act(T["OH%d" % k][:], T.ET[:].indirect(off), F.Copy, ["ET", "Y0U" if k == 0 else "LU%d" % ((k - 1) // 2)], ["OH%d" % k])
+
+    lo = [0]
+
+    def fused(items, reads):
+        need("g", deps("g", reads, []))
+        tr = []
+        for c, e, i, o, s in items:
+            rid, pid = topo.addr(c, core)
+            tr.append(RemoteDMATransfer(dst_ids=[DstId(rid=rid, pnc=pid)], dma_engine_mask=sum(1 << b for b in e),
+                                        remote_sem=T.sem[s], src=i, dst=o))
+            lo[0] += len(e)
+        g.remote_dma_fused(tr, local_sem=T.sem.lo)
+
+    on = topo.engines(core, relays[0])
+    direct = cores[(rank - 2) % n]
+    off = topo.engines(core, direct)
+    hi = [e for e in on if e not in off]
+
+    def tabs(nm, i):
+        return T[nm][:, 512 * i:512 * i + 512]
+
+    def piece(d):
+        s = (rank - d) % n
+        return T.LTS[:, 96 * s:96 * s + 96]
+
+    def half(a, key):
+        fused([(relays[a], on[0:8], tabs("J0", a), tabs("J0", a), "rJ"),
+               (relays[a + 1], on[8:16], tabs("J0", a + 1), tabs("J0", a + 1), "rJ")], [key])
+
+    half(0, "J0a")
+    fused([(direct, off[0:2], piece(2), T.LTA[:, 192:288], "aL2"), (relays[0], hi[0:4], piece(1), T.LI1[:], "rL"),
+           (relays[2], hi[4:8], piece(3), T.LI1[:], "rL")], ["LTS"])
+    half(2, "J0b")
+    fused([(relays[i], on[4 * i:4 * i + 4], tabs("C0", i), tabs("C0", i), "rC") for i in range(4)], ["C0"])
+
+    iota(T.D0S[:], [[0, 2304]], 0, 0, ["D0S"])
+    iota(T.D0S[:, 0:2304:3], [[0, 768]], -1000, 0, ["D0S"])
+    iota(T.D1S[:], [[0, 2304]], -255, 0, ["D1S"])
+    iota(T.IR[0:1, :], [[0, 24], [-1, 16]], 15, 0, ["IR"])
+    iota(T.PAT[:], [[0, 384]], 0, 0, ["PAT"])
+    iota(T.PAT[:, 0:384:16], [[0, 24]], -16384, 0, ["PAT"])
+    iota(T.EBA[0:48, :], [[0, 768]], 1, 0, ["EBA"])
+    op("g", lambda: g.affine_select(T.EBB[0:48, :], T.EBA[0:48, :], [[1, 768]], A.is_ge, 0.0, 0, -16), ["EBA"], ["EBB"])
+    op("g", lambda: g.affine_select(T.EBC[0:48, :], T.EBB[0:48, :], [[-1, 768]], A.is_ge, 0.0, 15, 16), ["EBB"], ["EBC"])
+
+    cp(T.STU[:], T.STI[:], ["STI"], ["STU"])
+    starts(0)
+    cp(T.Y0U[:], T.Y0W[:, 0:48], ["Y0W"], ["Y0U"])
+    onehot(0)
+    letters(0)
+    onehot(1)
+    onehot(2)
+    starts2(0)
+    ts(T.JW[:], T.JR[:], T.PC[:, 0:1], None, A.add, None, ["JR", "PC"], ["JW"])
+    ts(T.P15[:, 0:1], T.PC[:, 0:1], -1.0, 15.0, A.mult, A.add, ["PC"], ["P15"])
+    ts(T.B5[:], T.JW[:], 5.0, BIG, A.mult, A.add, ["JW"], ["B5"])
+    ts(T.DD[:], T.JW[:], 3.0, 15362.0, A.mult, A.add, ["JW"], ["DD"])
+    starts(1)
+    ts(T.IDB[:], T.IV[:], 0.0, None, A.is_equal, None, ["IV"], ["IDB"])
+    ts(T.ID16[:], T.IV[:], 0.0, 16.0, A.is_equal, A.mult, ["IV"], ["ID16"])
+    ts(T.SBX[:], T.SBB[:], T.PC[:, 0:1], None, A.mult, None, ["SBB", "PC"], ["SBX"])
+    starts2(1)
+    fill(T.D0A[:], 0.0, ["D0A"])
+    fill(T.D0A[:, 0:3840:5], -1000.0, ["D0A"])
+    D1K = ["D1_0", "D1_1"]
+    fill(T.D1[:], -255.0, D1K)
+
+    XP = ["XA", "XB"]
+    KP = ["KA", "KBK"]
+
+    def jkeys(d):
+        return ["J0a", "J0b", "Jz0"] if d == 0 else ["J%d" % d, "Jz%d" % d]
+
+    def walk(t, gaps):
+        slots = list(range(1 - t, 9))
+        first = slots[0]
+        ZN, ZZN = "Z%d" % t, "ZZ%d" % t
+        MK = "M%d" % t
+        M = T[MK]
+
+        def zk(k):
+            return "%s_%d" % (ZN, k)
+
+        def step_j(k):
+            if k < first:
+                d, offs, oh, rd = 0, blk("OFS", t), (T.OH0 if t == 0 else T.OHY), ["OFS%d" % t, "OH0" if t == 0 else "OHY"]
+            else:
+                d, offs, oh, rd = (k - 1) // 2 if k else 0, T.OFJ[:], T["OH%d" % k], ["OFJ", "OH%d" % k]
+            m = "MJ%d" % (k % 2)
+            tt(T[m][:], T["J%d" % d][:, 0:2056].indirect(offs), oh[:], A.mult, rd + jkeys(d), [m])
+
+        def step_x(k):
+            X = XP[k % 2]
+            o = T[X][:, 0:48]
+            m = "MJ%d" % (k % 2)
+            items = [(o, T.IDF[:], blk(ZN, k + 1), ["IDF", zk(k + 1)])] if k < 8 else []
+            items += sels(o, m, m)
+            if k >= first:
+                b = "BE%d" % (k % 2)
+                items.append((o, T.IDF[:], T[b][:], ["IDF", b]))
+            pe(items, [X])
+
+        def step_off(k):
+            X = XP[k % 2]
+            if k < 8:
+                b = "BE%d" % ((k + 1) % 2)
+                ts(T.OFJ[:], T[X][:, 0:48], 2048.0, None, A.min, None, [X], ["OFJ"])
+                ts(T[b][:], T[X][:, 0:48], -4096.0, 0.0, A.add, A.max, [X], [b])
+
+        def step_c(k):
+            X, a, o = XP[k % 2], "TC%d" % (k % 2), "OC%d" % (k % 2)
+            if k < first:
+                tt(T[a][:], T[X][:, 0:48], blk(ZN, first), A.subtract, [X, zk(first)], [a])
+            else:
+                tt(T[a][:], T[X][:, 0:48], blk(ZZN, k), A.add, [X, "%s_%d" % (ZZN, k)], [a])
+            ts(T[o][:], T[a][:], 2048.0, None, A.min, None, [a], [o])
+            d = (k - 1) // 2 if k >= max(first, 1) else 0
+            win = T["C%d" % d][:, 0:2056].indirect(T[o][:])
+            rd = ["C%d" % d, "Cz%d" % d, o]
+            if k < first:
+                act(T.D1[:, 0:3840:5], win, F.Copy, rd, D1K, scale=-1.0)
+            elif k == 8:
+                act(T.D0S[:, 1:2304:3], win, F.Copy, rd, ["D0S"])
+            else:
+                b = "D0A" if (k // 2) % 2 == 0 else "D0B"
+                act(T[b][:, 1 + 2 * (k % 2):3840:5], win, F.Copy, rd, [b])
+
+        def scan(gr, hf):
+            if gr == 4:
+                a, w, x, y, dk = 1152 * hf, 1152, T.D0S, T.D1S, ["D0S", "D1S"]
+            else:
+                a, w, x, y, dk = 1920 * hf, 1920, (T.D0A, T.D0B)[gr % 2], T.D1, [("D0A", "D0B")[gr % 2], "D1_%d" % hf]
+            b = 3840 * gr + a
+            op("v", lambda: g.vector.tensor_tensor_scan(T.OUT[:, b:b + w], x[:, a:a + w], y[:, a:a + w], 0.0, A.subtract, A.max),
+               dk, ["OUT%d_%d" % (gr, hf)])
+
+        def carry(gr, hf, q):
+            a = 3840 * (gr - 1) + 1920 * hf
+            src = T.OUT[:, a + 4:a + 1920:5]
+            if gr == 4:
+                out, w = T.D1S[:, 1152 * hf:1152 * hf + 1152:3], ["D1S"]
+            else:
+                out, w = T.D1[:, 1920 * hf:1920 * hf + 1920:5], ["D1_%d" % hf]
+            rd = ["OUT%d_%d" % (gr - 1, hf)]
+            if q == "v":
+                cp(out, src, rd, w)
+            else:
+                act(out, src, F.Copy, rd, w)
+
+        how = {}
+
+        def sign(k, q):
+            gr = k // 2
+            if k == 8:
+                src = T.OUT[:, 15362:OUTW:3]
+            else:
+                src = T.OUT[:, 3840 * gr + 2 + 2 * (k % 2):3840 * gr + 3840:5]
+            rd, s = ["OUT%d_0" % gr, "OUT%d_1" % gr], "SG%d" % (k % 4)
+            how[k] = q
+            if q == "v":
+                ts(T[s][:], src, 0.0, -1.0, A.is_gt, A.mult, rd, [s])
+            else:
+                act(T[s][:], src, F.Sign, rd, [s], bias=0.5, scale=-1.0)
+
+        def count(k):
+            if k < first:
+                return
+            o, s = T[KP[k % 2]][:, 0:48], "SG%d" % (k % 4)
+            pe([(o, T.IDF[:], blk(ZN, k), ["IDF", zk(k)])] + sels(o, s, s, "SBB"), [KP[k % 2]])
+
+        def judge(k):
+            if k < first:
+                return
+            p = KP[k % 2]
+            thr = -8.5 if how[k] == "v" else -1.0
+            if k == first:
+                ts(M[:], T[p][:, 0:48], thr, QK[k], A.is_lt, A.mult, [p], [MK])
+            else:
+                ts(T.EE[:], T[p][:, 0:48], thr, QK[k], A.is_lt, A.mult, [p], ["EE"])
+                tt(M[:], M[:], T.EE[:], A.max, [MK, "EE"], [MK])
+            if k < 8:
+                leave(k)
+
+        def leave(k):
+            if t == 0:
+                return
+            ts(T.DL[:], M[:], QK[k], 16.0, A.is_equal, A.mult, [MK], ["DL"])
+            if k == 0:
+                ts(T.DM[:], T.M0[:], 0.5, 16.0, A.is_gt, A.mult, ["M0"], ["DM"])
+                tt(T.DL[:], T.DL[:], T.DM[:], A.max, ["DL", "DM"], ["DL"])
+                tt(T.YI0[:, 0:48], T.Y0W[:, 0:48], T.DL[:], A.max, ["Y0W", "DL"], ["YI0"])
+                return
+            tt(blk("LF", k - 1), blk("LT1", k - 1), T.DL[:], A.max, ["LT1", "DL"], ["LF%d" % k])
+            d = (k - 1) // 2
+            if k % 2 == 0 and d:
+                rd = ks("LF", (k - 1, k))
+                src = T.LF[:, 96 * d:96 * d + 96]
+                if d == 2:
+                    fused([(cores[(rank + 2) % n], off[0:2], src, T.LI2[:], "aF2")], rd)
+                else:
+                    fused([(relays[0 if d == 3 else 2], hi[0:8], src, T.LI2[:], "rF")], rd)
+
+        step_j(first - 1)
+        step_x(first - 1)
+        for f in gaps.get(first - 1, []):
+            f()
+        step_off(first - 1)
+        step_c(first - 1)
+        cq = "v" if t == 0 else "s"
+        late = []
+        for k in slots:
+            step_j(k)
+            for f in late:
+                f()
+            late = []
+            step_x(k)
+            if k >= 5:
+                judge(k - 5)
+            for kk in {4: [0], 5: [1], 6: [2], 7: [3], 8: [4, 5]}.get(k, []):
+                count(kk)
+            if k >= 2:
+                gr, hf = (k - 2) // 2, k % 2
+                scan(gr, hf)
+                if gr == 3:
+                    carry(4, hf, "v")
+                elif cq == "v":
+                    carry(gr + 1, hf, "v")
+            for f in gaps.get(k, []):
+                f()
+            step_off(k)
+            if k % 2 == 1 or k == 8:
+                step_c(k)
+            else:
+                late.append(lambda k=k: step_c(k))
+            if k >= 2 and cq == "s" and k < 8:
+                late.append(lambda k=k: carry((k - 2) // 2 + 1, k % 2, "s"))
+            if k in (3, 5):
+                late.append(lambda k=k: k - 3 >= first and sign(k - 3, "s"))
+            if k in (4, 6):
+                late.append(lambda k=k: sign(k - 3, "s"))
+            if k == 7:
+                late.append(lambda: (sign(4, "s"), sign(5, "s")))
+        scan(3, 1)
+        carry(4, 1, "v")
+        sign(6, "v")
+        sign(7, "s")
+        judge(4)
+        scan(4, 0)
+        scan(4, 1)
+        sign(8, "v")
+        for k in (6, 7):
+            count(k)
+            judge(k - 1)
+        count(8)
+        judge(7)
+        judge(8)
+        tt(T.T1[:], T.B5[:], M[:], A.subtract, ["B5", MK], ["T1"])
+        tt(T.T2[:], T.T1[:], T.DD[:], A.min, ["T1", "DD"], ["T2"])
+        cp(T.SEL[:], T.T2[:], ["T2"], ["SEL"])
+        leave(8)
+        outs = ["OUT%d_%d" % (gr, hf) for gr in range(5) for hf in range(2)]
+        for hf in range(2):
+            ts(T.VF[:, 384 * hf:384 * hf + 384], T.OUT[:, 0:OUTW].indirect(T.SEL[:, 24 * hf:24 * hf + 24]), -1.0, None, A.mult, None,
+               ["SEL"] + outs, ["VF%d" % hf])
+
+    def lettergap(d):
+        letters(d)
+        onehot(2 * d + 1)
+        onehot(2 * d + 2)
+
+    def d0b():
+        fill(T.D0B[:], 0.0, ["D0B"])
+        fill(T.D0B[:, 0:3840:5], -1000.0, ["D0B"])
+
+    walk(0, {0: [d0b], 1: [lambda: lettergap(1)], 3: [lambda: lettergap(2)], 5: [lambda: lettergap(3)]})
+
+    for hf in range(2):
+        base = 512 * hf
+        pe([(T.KEY[:, base:base + 384], T.ONE[0:1, :], T.IR[0:1, :], ["ONE", "IR"])] +
+           [(T.KEY[:, base + 128 * b:base + 128 * b + 128], T.VF[:, 384 * hf + 128 * b:384 * hf + 128 * b + 128], T.ID16[:], ["VF%d" % hf, "ID16"])
+            for b in range(3)], ["KEY%d" % hf])
+    S8 = range(1, 9)
+    for k in S8:
+        ts(blk("ZD", k), T.M0[:], QK[k], 4096.0, A.is_equal, A.mult, ["M0"], ["ZD%d" % k])
+    ts(blk("Z1", 0), T.M0[:], 0.5, 4096.0, A.is_gt, A.mult, ["M0"], ["Z1_0"])
+    for hf in range(2):
+        op("v", lambda hf=hf: g.vector.tensor_tensor_scan(T.KM[:, 384 * hf:384 * hf + 384], T.PAT[:], T.KEY[:, 512 * hf:512 * hf + 384],
+                                                         0.0, A.add, A.max), ["PAT", "KEY%d" % hf], ["KM%d" % hf])
+    cp(T.KI[:], T.KM[:, 15:768:16], ["KM0", "KM1"], ["KI"])
+    ts(T.KB[:], T.KI[:], 15, None, A.bitwise_and, None, ["KI"], ["KB"])
+    cp(T.KC[:], T.KB[:], ["KB"], ["KC"])
+    pe([(T.XA[0:48, 0:128], T.KC[:], T.IDB[:], ["KC", "IDB"])], ["XA"])
+    cp(T.YT[0:48, :], T.XA[0:48, 0:128], ["XA"], ["YT"])
+    for hf in range(2):
+        for b in range(3):
+            q = 3 * hf + b
+            pe([(T.YB[:, 512 * hf + 128 * b:512 * hf + 128 * b + 128], T.EBC[0:48, 128 * q:128 * q + 128], T.YT[0:48, :], ["EBC", "YT"])],
+               ["YB%d" % hf])
+    Z1K = ks("Z1_", range(9))
+    tt(blk("Z1", 1, 8), blk("Z0", 1, 8), blk("ZD", 1, 8), A.add, ks("ZD", S8) + ks("Z0_", S8), Z1K[1:])
+    for hf in range(2):
+        ts(T.OHY[:, 384 * hf:384 * hf + 384], T.YB[:, 512 * hf:512 * hf + 384], T.P15[:, 0:1], None, A.is_equal, None,
+           ["YB%d" % hf, "P15"], ["OHY"])
+
+    def marks():
+        ts(T.Z12[:], T.Z1[:], 2.0, None, A.mult, None, Z1K, ["Z12"])
+        tt(blk("ZZ1", 0, 8), blk("Z12", 0, 8), blk("Z1", 1, 8), A.subtract, ["Z12"] + Z1K, ks("ZZ1_", range(8)))
+        cp(blk("ZZ1", 8), blk("Z12", 8), ["Z12"], ["ZZ1_8"])
+
+    def kept():
+        ts(T.LZ[:], blk("Z1", 1, 8), 1.0 / 256.0, None, A.mult, None, Z1K, ["LZ"])
+        tt(T.LT1[:], T.LTA[:], T.LZ[:], A.max, ["LZ"] + ks("LTA", range(4)), ["LT1"])
+
+    def newword():
+        pe(sels(T.YB[:, 0:48], "OHY", "OHY", "SBX"), ["YB0"])
+
+    def newword2():
+        cp(T.Y1W[:], T.YB[:, 0:48], ["YB0"], ["Y1W"])
+
+    walk(1, {-1: [marks], 1: [kept, newword], 2: [newword2]})
+
+    ts(T.DM[:], T.M1[:], 0.5, 16.0, A.is_gt, A.mult, ["M1"], ["DM"])
+    tt(T.YI1[:, 0:48], T.Y1W[:], T.DM[:], A.max, ["Y1W", "DM"], ["YI1"])
+    for h in range(16):
+        out, src = T.VN[:, 48 * h:48 * h + 48], T.VF[:, h:768:16]
+        if h % 2:
+            act(out, src, F.Copy, ["VF0", "VF1"], ["VN%d" % h])
+        else:
+            cp(out, src, ["VF0", "VF1"], ["VN%d" % h])
+    total = 16 * 11
+    dma("y", T.yi[:, 0:768], T.YI0[:, 0:48], "dO", total, ["YI0"], ["o1"])
+    for l in range(2):
+        a = (rank * 2 + l) * 768
+        dma("y", T.yl[:, a:a + 768], T.LF[:, 48 * l:48 * l + 48], "dO", total, ["LF%d" % (l + 1)], ["o2%d" % l])
+
+    def home(d):
+        s = (rank - d) % n
+        nm = "aF%d" % d
+        k = 2 if d == 2 else 8
+        lastw["LI%d" % d] = (nm, k, {nm: k})
+        for l in range(2):
+            a = (s * 2 + l) * 768
+            dma("y", T.yl[:, a:a + 768], T["LI%d" % d][:, 48 * l:48 * l + 48], "dO", total, ["LI%d" % d], ["o3%d%d" % (d, l)])
+
+    home(1)
+    home(2)
+    dma("y", T.yi[:, 768:1536], T.YI1[:, 0:48], "dO", total, ["YI1"], ["o4"])
+    dma("y", T.yv[:], T.VN[:], "dO", total, ks("VN", range(16)), ["o5"])
+    home(3)
+    g.sync.wait_ge(T.sem.dO, total)
+    for s, v in (("lo", lo[0]), ("qv", cnt["v"]), ("qs", cnt["s"]), ("qp", cnt["p"]), ("qg", cnt["g"]), ("dLr", 96)):
+        g.wait_ge(T.sem[s], v)

@@ -2,16 +2,16 @@ from concourse.bass import DstId, RemoteDMATransfer
 from concourse.mybir import AluOpType as A, ActivationFunctionType as F
 
 OUTW = 4 * 3840 + 2304
-SCRATCH = {}
+SCRATCH = {"LTD": ("dram", [8, 128, 48], "bfloat16")}
 for _ty, _s in (
-        ("bfloat16", "C0 2064 C1 2064 C2 2064 C3 2064 OHY 768 SG0 768 SG1 768 SG2 768 SG3 768 D0A 3840 D0B 3840 D1 3840 D0S 2304 D1S 2304 "
-         "VF 768 VN 768 LTA 384 LTS 384 LF 384 LT1 384 LZ 384 LI1 96 LI2 96 LI3 96 Y0W 64 YI0 64 YI1 64 KC 48 YT 128 ET 32 IDB 128 ID16 128 "
+        ("bfloat16", "C0 2064 C1 2064 C2 2064 C3 2064 OHY 768 SG0 1536 SG1 1536 D0A 3840 D0B 3840 D1 3840 D0S 2304 D1S 2304 "
+         "VF 768 VN 768 LTA 384 LF 384 LT1 384 LZ 384 LI1 96 LI2 96 LI3 96 Y0W 64 YI0 64 YI1 64 KC 48 YT 128 ET 32 IDB 128 ID16 128 "
          "SBB 144 SBX 144 EBA 768 EBB 768 EBC 768 IR 384 ONE 128 PAT 384 OUT %d " % OUTW + " ".join("OH%d 768" % k for k in range(9))),
         ("int32", "J0 2056 J1 2056 J2 2056 J3 2056 STI 96 KI 48 KB 48 PI 8 PJ 8"),
         ("float16", "MJ0 768 MJ1 768 STF 768 BE0 48 BE1 48 Z0 432 Z02 432 Z1 432 Z12 432 ZD 432 IDF 128 SBF 144"),
         ("uint16", "STU 96 OFS 96 OFJ 48 OC0 48 OC1 48 LU 384 Y0U 48 SEL 48"),
-        ("float32", "KM 768 IOT 2048 TC0 48 TC1 48 Y1W 48 ZZ0 432 ZZ1 432 M0 48 M1 48 EE 48 DL 48 DM 48 T1 48 T2 48 PC 8 P15 8 V8 8 V8A 8 V8B 8 "
-         "XR 32 JR 48 JW 48 B5 48 DD 48 IV 128"),
+        ("float32", "KM 768 IOT 2048 TC0 48 TC1 48 Y1W 48 ZZ0 432 ZZ1 432 M0 48 M1 48 EE 48 EF 48 LD 432 DL 48 DM 48 T1 48 T2 48 PC 8 P15 8 "
+         "V8 8 V8A 8 V8B 8 XR 32 JR 48 JW 48 B5 48 DD 48 IV 128"),
         ("psum", "XA 512 XB 512 KA 512 KBK 512 KEY 1024 YB 1024")):
     _p = _s.split()
     for _n, _w in zip(_p[::2], _p[1::2]):
@@ -181,18 +181,17 @@ def rank_program(g, core, T, topo):
 
     dma("y", T.STI[:], T.st[:], "dSt", 16, [], ["STI"])
     dma("s", T.J0[:, 0:1024], T.jm[:, 0:1024], "dJA", 16, [], ["J0a"])
-    for l in range(2):
-        a = (rank * 2 + l) * 768
-        dma("y", T.LTA[:, 48 * l:48 * l + 48], T.lt[:, a:a + 768], "dLo", 48, [], ["LTA0"])
     dma("y", T.Y0W[:, 0:48], T.y0[:], "dLo", 48, [], ["Y0W"])
-    dma("s", T.J0[:, 1024:2048], T.jm[:, 1024:2048], "dJB", 16, [], ["J0b"])
-    dma("s", T.C0[:, 0:2048], T.cf[:], "dC", 16, [], ["C0"])
     for d in range(1, n):
         s = (rank - d) % n
         for l in range(2):
             a = (s * 2 + l) * 768
-            b = 96 * s + 48 * l
-            dma("y", T.LTS[:, b:b + 48], T.lt[:, a:a + 768], "dLr", 96, [], ["LTS"])
+            dma("s", T.LTD[2 * s + l], T.lt[:, a:a + 768], "dLr", 96, [], ["LTS"])
+    for l in range(2):
+        a = (rank * 2 + l) * 768
+        dma("y", T.LTA[:, 48 * l:48 * l + 48], T.lt[:, a:a + 768], "dLo", 48, [], ["LTA0"])
+    dma("y", T.J0[:, 1024:2048], T.jm[:, 1024:2048], "dJB", 16, [], ["J0b"])
+    dma("s", T.C0[:, 0:2048], T.cf[:], "dC", 16, [], ["C0"])
     for d in range(1, n):
         for a, w, k in (("aJ", "J", 32), ("aC", "C", 32), ("aL", "LTA", 8 if d != 2 else 2)):
             nm = "%s%d" % (a, d)
@@ -275,17 +274,16 @@ def rank_program(g, core, T, topo):
     def tabs(nm, i):
         return T[nm][:, 512 * i:512 * i + 512]
 
-    def piece(d):
-        s = (rank - d) % n
-        return T.LTS[:, 96 * s:96 * s + 96]
+    def piece(c, e, d, out, a, sem):
+        return [(c, e[l::2], T.LTD[2 * ((rank - d) % n) + l], T[out][:, a + 48 * l:a + 48 * l + 48], sem) for l in range(2)]
 
     def half(a, key):
         fused([(relays[a], on[0:8], tabs("J0", a), tabs("J0", a), "rJ"),
                (relays[a + 1], on[8:16], tabs("J0", a + 1), tabs("J0", a + 1), "rJ")], [key])
 
     half(0, "J0a")
-    fused([(direct, off[0:2], piece(2), T.LTA[:, 192:288], "aL2"), (relays[0], hi[0:4], piece(1), T.LI1[:], "rL"),
-           (relays[2], hi[4:8], piece(3), T.LI1[:], "rL")], ["LTS"])
+    fused(piece(direct, off[0:2], 2, "LTA", 192, "aL2") + piece(relays[0], hi[0:4], 1, "LI1", 0, "rL") +
+          piece(relays[2], hi[4:8], 3, "LI1", 0, "rL"), ["LTS"])
     half(2, "J0b")
     fused([(relays[i], on[4 * i:4 * i + 4], tabs("C0", i), tabs("C0", i), "rC") for i in range(4)], ["C0"])
 
@@ -299,8 +297,16 @@ def rank_program(g, core, T, topo):
     op("g", lambda: g.affine_select(T.EBB[0:48, :], T.EBA[0:48, :], [[1, 768]], A.is_ge, 0.0, 0, -16), ["EBA"], ["EBB"])
     op("g", lambda: g.affine_select(T.EBC[0:48, :], T.EBB[0:48, :], [[-1, 768]], A.is_ge, 0.0, 15, 16), ["EBB"], ["EBC"])
 
+    def holes(nm, zeros):
+        fill(T[nm][:, 0:3840:5], -1000.0, [nm + "c0"])
+        for i in zeros:
+            fill(T[nm][:, i:3840:5], 0.0, [nm + "c%d" % i])
+
+    D1K = ["D1_0", "D1_1"]
+    fill(T.D1[:], -255.0, D1K)
     cp(T.STU[:], T.STI[:], ["STI"], ["STU"])
     starts(0)
+    holes("D0A", (1, 2, 4))
     cp(T.Y0U[:], T.Y0W[:, 0:48], ["Y0W"], ["Y0U"])
     onehot(0)
     letters(0)
@@ -311,15 +317,9 @@ def rank_program(g, core, T, topo):
     ts(T.P15[:, 0:1], T.PC[:, 0:1], -1.0, 15.0, A.mult, A.add, ["PC"], ["P15"])
     ts(T.B5[:], T.JW[:], 5.0, BIG, A.mult, A.add, ["JW"], ["B5"])
     ts(T.DD[:], T.JW[:], 3.0, 15362.0, A.mult, A.add, ["JW"], ["DD"])
-    starts(1)
     ts(T.IDB[:], T.IV[:], 0.0, None, A.is_equal, None, ["IV"], ["IDB"])
     ts(T.ID16[:], T.IV[:], 0.0, 16.0, A.is_equal, A.mult, ["IV"], ["ID16"])
     ts(T.SBX[:], T.SBB[:], T.PC[:, 0:1], None, A.mult, None, ["SBB", "PC"], ["SBX"])
-    starts2(1)
-    fill(T.D0A[:], 0.0, ["D0A"])
-    fill(T.D0A[:, 0:3840:5], -1000.0, ["D0A"])
-    D1K = ["D1_0", "D1_1"]
-    fill(T.D1[:], -255.0, D1K)
 
     XP = ["XA", "XB"]
     KP = ["KA", "KBK"]
@@ -361,14 +361,20 @@ def rank_program(g, core, T, topo):
             if k < 8:
                 b = "BE%d" % ((k + 1) % 2)
                 ts(T.OFJ[:], T[X][:, 0:48], 2048.0, None, A.min, None, [X], ["OFJ"])
+                step_c1(k)
                 ts(T[b][:], T[X][:, 0:48], -4096.0, 0.0, A.add, A.max, [X], [b])
+            else:
+                step_c1(k)
 
-        def step_c(k):
-            X, a, o = XP[k % 2], "TC%d" % (k % 2), "OC%d" % (k % 2)
+        def step_c1(k):
+            X, a = XP[k % 2], "TC%d" % (k % 2)
             if k < first:
                 tt(T[a][:], T[X][:, 0:48], blk(ZN, first), A.subtract, [X, zk(first)], [a])
             else:
                 tt(T[a][:], T[X][:, 0:48], blk(ZZN, k), A.add, [X, "%s_%d" % (ZZN, k)], [a])
+
+        def step_c(k):
+            a, o = "TC%d" % (k % 2), "OC%d" % (k % 2)
             ts(T[o][:], T[a][:], 2048.0, None, A.min, None, [a], [o])
             d = (k - 1) // 2 if k >= max(first, 1) else 0
             win = T["C%d" % d][:, 0:2056].indirect(T[o][:])
@@ -385,7 +391,9 @@ def rank_program(g, core, T, topo):
             if gr == 4:
                 a, w, x, y, dk = 1152 * hf, 1152, T.D0S, T.D1S, ["D0S", "D1S"]
             else:
-                a, w, x, y, dk = 1920 * hf, 1920, (T.D0A, T.D0B)[gr % 2], T.D1, [("D0A", "D0B")[gr % 2], "D1_%d" % hf]
+                nm = ("D0A", "D0B")[gr % 2]
+                a, w, x, y = 1920 * hf, 1920, T[nm], T.D1
+                dk = [nm + e for e in ("", "c0", "c2", "c4") + (() if gr % 2 else ("c1",))] + ["D1_%d" % hf]
             b = 3840 * gr + a
             op("v", lambda: g.vector.tensor_tensor_scan(T.OUT[:, b:b + w], x[:, a:a + w], y[:, a:a + w], 0.0, A.subtract, A.max),
                dk, ["OUT%d_%d" % (gr, hf)])
@@ -405,56 +413,63 @@ def rank_program(g, core, T, topo):
 
         how = {}
 
-        def sign(k, q):
-            gr = k // 2
+        def sign(k, q, hf):
+            if k < first:
+                return
+            gr, a = k // 2, 768 * (k % 2) + 384 * hf
             if k == 8:
-                src = T.OUT[:, 15362:OUTW:3]
+                src = T.OUT[:, 15362 + 1152 * hf:15360 + 1152 * hf + 1152:3]
             else:
-                src = T.OUT[:, 3840 * gr + 2 + 2 * (k % 2):3840 * gr + 3840:5]
-            rd, s = ["OUT%d_0" % gr, "OUT%d_1" % gr], "SG%d" % (k % 4)
+                b = 3840 * gr + 1920 * hf
+                src = T.OUT[:, b + 2 + 2 * (k % 2):b + 1920:5]
+            rd, o = ["OUT%d_%d" % (gr, hf)], T["SG%d" % (gr % 2)][:, a:a + 384]
+            w = ["SG%d_%d%d" % (gr % 2, k % 2, hf)]
             how[k] = q
             if q == "v":
-                ts(T[s][:], src, 0.0, -1.0, A.is_gt, A.mult, rd, [s])
+                ts(o, src, 0.0, -1.0, A.is_gt, A.mult, rd, w)
             else:
-                act(T[s][:], src, F.Sign, rd, [s], bias=0.5, scale=-1.0)
+                act(o, src, F.Sign, rd, w, bias=0.5, scale=-1.0)
 
-        def count(k):
-            if k < first:
-                return
-            o, s = T[KP[k % 2]][:, 0:48], "SG%d" % (k % 4)
-            pe([(o, T.IDF[:], blk(ZN, k), ["IDF", zk(k)])] + sels(o, s, s, "SBB"), [KP[k % 2]])
+        def count(gr):
+            k0, k1 = max(2 * gr, first), min(2 * gr + 1, 8)
+            m, p, a = k1 - k0 + 1, gr % 2, 768 * (k0 % 2)
+            o = T[KP[p]][:, 0:48 * m]
+            rd = ["SG%d_%d%d" % (p, k % 2, hf) for k in range(k0, k1 + 1) for hf in (0, 1)] + ["SBB"]
+            pe([(o, T.IDF[:], blk(ZN, k0, m), ["IDF"] + [zk(k) for k in range(k0, k1 + 1)])] +
+               [(o, T.SBB[:, 15 - h:143 - h], T["SG%d" % p][:, a + h:a + 768 * m:16], rd) for h in range(16)], [KP[p]])
 
-        def judge(k):
-            if k < first:
-                return
-            p = KP[k % 2]
-            thr = -8.5 if how[k] == "v" else -1.0
-            if k == first:
-                ts(M[:], T[p][:, 0:48], thr, QK[k], A.is_lt, A.mult, [p], [MK])
-            else:
-                ts(T.EE[:], T[p][:, 0:48], thr, QK[k], A.is_lt, A.mult, [p], ["EE"])
-                tt(M[:], M[:], T.EE[:], A.max, [MK, "EE"], [MK])
-            if k < 8:
-                leave(k)
+        def judge1(gr):
+            p = KP[gr % 2]
+            k0, k1 = max(2 * gr, first), min(2 * gr + 1, 8)
+            for k in range(k0, k1 + 1):
+                out, w = (M, MK) if k == first else (T.EE, "EE") if k % 2 == 0 else (T.EF, "EF")
+                thr = -8.5 if how[k] == "v" else -1.0
+                ts(out[:], T[p][:, 48 * (k - k0):48 * (k - k0) + 48], thr, QK[k], A.is_lt, A.mult, [p], [w])
 
-        def leave(k):
+        def judge2(gr):
+            for k in range(max(2 * gr, first + 1), min(2 * gr + 1, 8) + 1):
+                w = "EE" if k % 2 == 0 else "EF"
+                tt(M[:], M[:], T[w][:], A.max, [MK, w], [MK])
+
+        def leave(kk):
             if t == 0:
                 return
-            ts(T.DL[:], M[:], QK[k], 16.0, A.is_equal, A.mult, [MK], ["DL"])
-            if k == 0:
-                ts(T.DM[:], T.M0[:], 0.5, 16.0, A.is_gt, A.mult, ["M0"], ["DM"])
-                tt(T.DL[:], T.DL[:], T.DM[:], A.max, ["DL", "DM"], ["DL"])
-                tt(T.YI0[:, 0:48], T.Y0W[:, 0:48], T.DL[:], A.max, ["Y0W", "DL"], ["YI0"])
+            for k in kk:
+                ts(blk("LD", k), M[:], QK[k], 16.0, A.is_equal, A.mult, [MK], ["LD%d" % k])
+            if kk[0]:
+                a, m = kk[0] - 1, len(kk)
+                tt(blk("LF", a, m), blk("LT1", a, m), blk("LD", a + 1, m), A.max, ["LT1"] + ks("LD", kk), ks("LF", kk))
                 return
-            tt(blk("LF", k - 1), blk("LT1", k - 1), T.DL[:], A.max, ["LT1", "DL"], ["LF%d" % k])
-            d = (k - 1) // 2
-            if k % 2 == 0 and d:
-                rd = ks("LF", (k - 1, k))
-                src = T.LF[:, 96 * d:96 * d + 96]
-                if d == 2:
-                    fused([(cores[(rank + 2) % n], off[0:2], src, T.LI2[:], "aF2")], rd)
-                else:
-                    fused([(relays[0 if d == 3 else 2], hi[0:8], src, T.LI2[:], "rF")], rd)
+            ts(T.DM[:], T.M0[:], 0.5, 16.0, A.is_gt, A.mult, ["M0"], ["DM"])
+            tt(T.DL[:], blk("LD", 0), T.DM[:], A.max, ["LD0", "DM"], ["DL"])
+            tt(T.YI0[:, 0:48], T.Y0W[:, 0:48], T.DL[:], A.max, ["Y0W", "DL"], ["YI0"])
+
+        def goes(d):
+            rd, src = ks("LF", (2 * d + 1, 2 * d + 2)), T.LF[:, 96 * d:96 * d + 96]
+            if d == 2:
+                fused([(cores[(rank + 2) % n], off[0:2], src, T.LI2[:], "aF2")], rd)
+            else:
+                fused([(relays[0 if d == 3 else 2], hi[0:8], src, T.LI2[:], "rF")], rd)
 
         step_j(first - 1)
         step_x(first - 1)
@@ -462,7 +477,6 @@ def rank_program(g, core, T, topo):
             f()
         step_off(first - 1)
         step_c(first - 1)
-        cq = "v" if t == 0 else "s"
         late = []
         for k in slots:
             step_j(k)
@@ -470,65 +484,71 @@ def rank_program(g, core, T, topo):
                 f()
             late = []
             step_x(k)
-            if k >= 5:
-                judge(k - 5)
-            for kk in {4: [0], 5: [1], 6: [2], 7: [3], 8: [4, 5]}.get(k, []):
-                count(kk)
+            gr, hf = (k - 2) // 2, k % 2
+            due = {5: 0, 7: 1}.get(k)
+            if due is not None:
+                judge1(due)
             if k >= 2:
-                gr, hf = (k - 2) // 2, k % 2
                 scan(gr, hf)
-                if gr == 3:
-                    carry(4, hf, "v")
-                elif cq == "v":
+                if gr == 3 or t == 0:
                     carry(gr + 1, hf, "v")
+                if gr < 3 and t == 0:
+                    sign(2 * gr, "v", hf)
+                    sign(2 * gr + 1, "s", hf)
+            if due is not None:
+                judge2(due)
+            if k in (4, 6, 8):
+                count((k - 4) // 2)
             for f in gaps.get(k, []):
                 f()
             step_off(k)
-            if k % 2 == 1 or k == 8:
-                step_c(k)
-            else:
-                late.append(lambda k=k: step_c(k))
-            if k >= 2 and cq == "s" and k < 8:
-                late.append(lambda k=k: carry((k - 2) // 2 + 1, k % 2, "s"))
-            if k in (3, 5):
-                late.append(lambda k=k: k - 3 >= first and sign(k - 3, "s"))
-            if k in (4, 6):
-                late.append(lambda k=k: sign(k - 3, "s"))
-            if k == 7:
-                late.append(lambda: (sign(4, "s"), sign(5, "s")))
+            step_c(k)
+            if t == 0 and k < 7:
+                late.append(lambda k=k: onehot(k + 2))
+            if k >= 2 and t == 1 and k < 8:
+                late.append(lambda gr=gr, hf=hf: (carry(gr + 1, hf, "s"), sign(2 * gr, "s", hf), sign(2 * gr + 1, "s", hf)))
         scan(3, 1)
         carry(4, 1, "v")
-        sign(6, "v")
-        sign(7, "s")
-        judge(4)
+        for hf in range(2):
+            sign(6, "v", hf)
+            sign(7, "s", hf)
         scan(4, 0)
+        count(3)
+        judge1(2)
         scan(4, 1)
-        sign(8, "v")
-        for k in (6, 7):
-            count(k)
-            judge(k - 1)
-        count(8)
-        judge(7)
-        judge(8)
+        judge2(2)
+        if t:
+            sign(8, "v", 0)
+            sign(8, "v", 1)
+            count(4)
+            leave((1, 2, 3, 4))
+            goes(1)
+        judge1(3)
+        judge2(3)
+        if t:
+            judge1(4)
+            judge2(4)
+            leave((5, 6, 7, 8))
+            goes(3)
         tt(T.T1[:], T.B5[:], M[:], A.subtract, ["B5", MK], ["T1"])
         tt(T.T2[:], T.T1[:], T.DD[:], A.min, ["T1", "DD"], ["T2"])
         cp(T.SEL[:], T.T2[:], ["T2"], ["SEL"])
-        leave(8)
         outs = ["OUT%d_%d" % (gr, hf) for gr in range(5) for hf in range(2)]
         for hf in range(2):
             ts(T.VF[:, 384 * hf:384 * hf + 384], T.OUT[:, 0:OUTW].indirect(T.SEL[:, 24 * hf:24 * hf + 24]), -1.0, None, A.mult, None,
                ["SEL"] + outs, ["VF%d" % hf])
+            if hf == 0:
+                if t == 0:
+                    sign(8, "s", 0)
+                    sign(8, "s", 1)
+                    count(4)
+                else:
+                    goes(2)
+                    leave((0,))
+        return lambda: (judge1(4), judge2(4))
 
-    def lettergap(d):
-        letters(d)
-        onehot(2 * d + 1)
-        onehot(2 * d + 2)
-
-    def d0b():
-        fill(T.D0B[:], 0.0, ["D0B"])
-        fill(T.D0B[:, 0:3840:5], -1000.0, ["D0B"])
-
-    walk(0, {0: [d0b], 1: [lambda: lettergap(1)], 3: [lambda: lettergap(2)], 5: [lambda: lettergap(3)]})
+    fin = walk(0, {0: [lambda: holes("D0B", (2, 4))], 1: [lambda: letters(1), lambda: starts(1)], 2: [lambda: starts2(1)],
+                   3: [lambda: letters(2)], 5: [lambda: letters(3)]})
 
     for hf in range(2):
         base = 512 * hf
@@ -536,9 +556,6 @@ def rank_program(g, core, T, topo):
            [(T.KEY[:, base + 128 * b:base + 128 * b + 128], T.VF[:, 384 * hf + 128 * b:384 * hf + 128 * b + 128], T.ID16[:], ["VF%d" % hf, "ID16"])
             for b in range(3)], ["KEY%d" % hf])
     S8 = range(1, 9)
-    for k in S8:
-        ts(blk("ZD", k), T.M0[:], QK[k], 4096.0, A.is_equal, A.mult, ["M0"], ["ZD%d" % k])
-    ts(blk("Z1", 0), T.M0[:], 0.5, 4096.0, A.is_gt, A.mult, ["M0"], ["Z1_0"])
     for hf in range(2):
         op("v", lambda hf=hf: g.vector.tensor_tensor_scan(T.KM[:, 384 * hf:384 * hf + 384], T.PAT[:], T.KEY[:, 512 * hf:512 * hf + 384],
                                                          0.0, A.add, A.max), ["PAT", "KEY%d" % hf], ["KM%d" % hf])
@@ -552,14 +569,20 @@ def rank_program(g, core, T, topo):
             q = 3 * hf + b
             pe([(T.YB[:, 512 * hf + 128 * b:512 * hf + 128 * b + 128], T.EBC[0:48, 128 * q:128 * q + 128], T.YT[0:48, :], ["EBC", "YT"])],
                ["YB%d" % hf])
+    fin()
+    for k in S8:
+        ts(blk("ZD", k), T.M0[:], QK[k], 4096.0, A.is_equal, A.mult, ["M0"], ["ZD%d" % k])
+    ts(blk("Z1", 0), T.M0[:], 0.5, 4096.0, A.is_gt, A.mult, ["M0"], ["Z1_0"])
     Z1K = ks("Z1_", range(9))
-    tt(blk("Z1", 1, 8), blk("Z0", 1, 8), blk("ZD", 1, 8), A.add, ks("ZD", S8) + ks("Z0_", S8), Z1K[1:])
     for hf in range(2):
         ts(T.OHY[:, 384 * hf:384 * hf + 384], T.YB[:, 512 * hf:512 * hf + 384], T.P15[:, 0:1], None, A.is_equal, None,
            ["YB%d" % hf, "P15"], ["OHY"])
 
     def marks():
+        tt(blk("Z1", 1, 8), blk("Z0", 1, 8), blk("ZD", 1, 8), A.add, ks("ZD", S8) + ks("Z0_", S8), Z1K[1:])
         ts(T.Z12[:], T.Z1[:], 2.0, None, A.mult, None, Z1K, ["Z12"])
+
+    def marks2():
         tt(blk("ZZ1", 0, 8), blk("Z12", 0, 8), blk("Z1", 1, 8), A.subtract, ["Z12"] + Z1K, ks("ZZ1_", range(8)))
         cp(blk("ZZ1", 8), blk("Z12", 8), ["Z12"], ["ZZ1_8"])
 
@@ -573,7 +596,7 @@ def rank_program(g, core, T, topo):
     def newword2():
         cp(T.Y1W[:], T.YB[:, 0:48], ["YB0"], ["Y1W"])
 
-    walk(1, {-1: [marks], 1: [kept, newword], 2: [newword2]})
+    walk(1, {-1: [marks], 0: [marks2], 1: [kept, newword], 2: [newword2]})
 
     ts(T.DM[:], T.M1[:], 0.5, 16.0, A.is_gt, A.mult, ["M1"], ["DM"])
     tt(T.YI1[:, 0:48], T.Y1W[:], T.DM[:], A.max, ["Y1W", "DM"], ["YI1"])
@@ -599,9 +622,9 @@ def rank_program(g, core, T, topo):
             dma("y", T.yl[:, a:a + 768], T["LI%d" % d][:, 48 * l:48 * l + 48], "dO", total, ["LI%d" % d], ["o3%d%d" % (d, l)])
 
     home(1)
-    home(2)
     dma("y", T.yi[:, 768:1536], T.YI1[:, 0:48], "dO", total, ["YI1"], ["o4"])
     dma("y", T.yv[:], T.VN[:], "dO", total, ks("VN", range(16)), ["o5"])
+    home(2)
     home(3)
     g.sync.wait_ge(T.sem.dO, total)
     for s, v in (("lo", lo[0]), ("qv", cnt["v"]), ("qs", cnt["s"]), ("qp", cnt["p"]), ("qg", cnt["g"]), ("dLr", 96)):

from concourse.bass import DstId, RemoteDMATransfer
from concourse.mybir import AluOpType as A, ActivationFunctionType as F

OUTW = 4 * 3840 + 2304
SCRATCH = {"LTD": ("dram", [8, 128, 48], "bfloat16")}
for _ty, _s in (
        ("bfloat16", "C0 2064 C1 2064 C2 2064 C3 2064 OHY 768 SG0 1536 SG1 1536 D0A 3840 D0B 3840 D1 3840 D0S 2304 D1S 2304 "
         "VF 768 VN 768 LTA 384 LF 384 LT1 384 LZ 384 LI1 96 LI2 96 LI3 96 Y0W 64 YI0 64 YI1 64 KC 48 YT 128 ET 32 IDB 128 ID16 128 "
         "SBB 144 SBX 144 EBA 768 EBB 768 EBC 768 IR 384 ONE 128 PAT 384 OUT %d " % OUTW + " ".join("OH%d 768" % k for k in range(9))),
        ("int32", "J0 2056 J1 2056 J2 2056 J3 2056 STI 96 KI 48 KB 48 PI 8 PJ 8"),
        ("float16", "MJ0 768 MJ1 768 STF 768 BE0 48 BE1 48 Z0 432 Z02 432 Z1 432 Z12 432 ZD 432 IDF 128 SBF 144"),
        ("uint16", "STU 96 OFS 96 OFJ 48 OC0 48 OC1 48 LU 384 Y0U 48 SEL 48"),
        ("float32", "KM 768 IOT 2048 TC0 48 TC1 48 Y1W 48 ZZ0 432 ZZ1 432 M0 48 M1 48 EE 48 EF 48 LD 432 DL 48 DM 48 T1 48 T2 48 PC 8 P15 8 "
         "V8 8 V8A 8 V8B 8 XR 32 JR 48 JW 48 B5 48 DD 48 IV 128"),
        ("psum", "XA 512 XB 512 KA 512 KBK 512 KEY 1024 YB 1024")):
    _p = _s.split()
    for _n, _w in zip(_p[::2], _p[1::2]):
        SCRATCH[_n] = ("psum", [128, int(_w)], "float32") if _ty == "psum" else ("sbuf", [128, int(_w)], _ty)

SEMAPHORES = "qv qs qp qg dJA dJB dC dSt dLo dLr dO lo rJ rC rL rF".split()
SEMAPHORES += ["%s%d" % (a, d) for a in ("aJ", "aC", "aL", "aF") for d in (1, 2, 3)]

WORLD = 256
BIG = 40000.0
QK = [BIG - (3840 * (k // 2) + 2 + 2 * (k % 2)) for k in range(8)] + [1.0]


def routes(topo, cores, r):
    c, n = cores[r], len(cores)
    x1, x3 = cores[(r - 1) % n], cores[(r - 3) % n]
    own = [e for e in topo.cores_of(c) if e != c and topo.may_write(e, x1)]
    same = [e for e in own if topo.die(e) == topo.die(c)]
    oth = [e for e in own if topo.die(e) != topo.die(c)]
    relays = [same[0], oth[0], same[1], oth[1]]
    far = [e for e in range(WORLD) if topo.mates(e, x3) and topo.may_write(e, x3)]
    pick = []
    for e in relays:
        pick.append([y for y in far if topo.die(y) == topo.die(e) and y not in pick][0])
    return relays, pick


def hand_on(g, core, T, topo):
    cores, n = T.cores, len(T.cores)
    lo = [0]

    def send(dst, out, in_, sem):
        rid, pid = topo.addr(dst, core)
        g.remote_dma(out, in_, T.sem[sem], T.sem.lo, pid, rid, topo.mask(core, dst))
        lo[0] += len(topo.engines(core, dst))

    for r in range(n):
        relays, far = routes(topo, cores, r)
        if core in relays:
            i = relays.index(core)
            x = [cores[(r - d) % n] for d in range(n)]
            cs = slice(512 * i, 512 * i + 512)
            g.wait_ge(T.sem.rJ, 8)
            send(x[1], T.J1[:, cs], T.J0[:, cs], "aJ1")
            if i in (0, 2):
                d = 1 if i == 0 else 3
                g.wait_ge(T.sem.rL, 4)
                send(x[d], T.LTA[:, 96 * d:96 * d + 96], T.LI1[:], "aL%d" % d)
            g.wait_ge(T.sem.rC, 4)
            send(x[1], T.C1[:, cs], T.C0[:, cs], "aC1")
            send(x[2], T.J2[:, cs], T.J0[:, cs], "aJ2")
            send(far[i], T.J0[:, cs], T.J0[:, cs], "rJ")
            send(x[2], T.C2[:, cs], T.C0[:, cs], "aC2")
            send(far[i], T.C0[:, cs], T.C0[:, cs], "rC")
            if i in (0, 2):
                d = 3 if i == 0 else 1
                g.wait_ge(T.sem.rF, 8)
                send(cores[(r + d) % n], T["LI%d" % d][:], T.LI2[:], "aF%d" % d)
        if core in far:
            i = far.index(core)
            x3 = cores[(r - 3) % n]
            cs = slice(512 * i, 512 * i + 512)
            k = len(topo.engines(relays[i], core))
            g.wait_ge(T.sem.rJ, k)
            send(x3, T.J3[:, cs], T.J0[:, cs], "aJ3")
            g.wait_ge(T.sem.rC, k)
            send(x3, T.C3[:, cs], T.C0[:, cs], "aC3")
    if lo[0]:
        g.wait_ge(T.sem.lo, lo[0])


def rank_program(g, core, T, topo):
    rank = T.rank_of(core)
    if rank is None:
        hand_on(g, core, T, topo)
        return
    cores, n = T.cores, len(T.cores)
    relays, far = routes(topo, cores, rank)
    Q = {"v": g.vector, "s": g.scalar, "p": g.tensor, "g": g, "y": g.sync}
    SEM = {"v": "qv", "s": "qs", "p": "qp", "g": "qg"}
    cnt = {q: 0 for q in SEM}
    clock = {q: {} for q in Q}
    lastw, readers = {}, {}

    def need(q, toks):
        best = {}
        for t in toks:
            if t and clock[q].get(t[0], 0) < t[1] and (t[0] not in best or best[t[0]][1] < t[1]):
                best[t[0]] = t
        for t in sorted(best.values(), key=lambda t: -len(t[2])):
            if clock[q].get(t[0], 0) >= t[1]:
                continue
            Q[q].wait_ge(T.sem[t[0]], t[1])
            for s, v in t[2].items():
                if clock[q].get(s, 0) < v:
                    clock[q][s] = v

    def deps(q, reads, writes):
        out = [lastw.get(r) for r in reads]
        for w in writes:
            t = lastw.get(w)
            if t and not (q == "p" and t[0] == "qp"):
                out.append(t)
            out += readers.get(w, [])
        return out

    def done(tok, reads, writes):
        for r in reads:
            readers.setdefault(r, []).append(tok)
        for w in writes:
            lastw[w] = tok
            readers[w] = []

    def op(q, call, reads, writes):
        need(q, deps(q, reads, writes))
        cnt[q] += 1
        call().then_inc(T.sem[SEM[q]], 1)
        c = dict(clock[q])
        c[SEM[q]] = cnt[q]
        done((SEM[q], cnt[q], c), reads, writes)

    def pe(items, writes):
        allr = []
        for i, (o, l, r, rd) in enumerate(items):
            need("p", deps("p", rd, writes if i == 0 else []))
            allr += rd
            ins = g.tensor.matmul(o, l, r, i == 0, i == len(items) - 1)
        cnt["p"] += 1
        ins.then_inc(T.sem.qp, 1)
        c = dict(clock["p"])
        c["qp"] = cnt["p"]
        done(("qp", cnt["p"], c), allr, writes)

    def dma(q, out, in_, sem, total, reads, writes):
        need(q, [t for t in deps(q, reads, writes) if t and t[0] != sem])
        Q[q].dma_start(out, in_).then_inc(T.sem[sem], 16)
        c = dict(clock[q])
        c[sem] = total
        done((sem, total, c), reads, writes)

    def ts(out, in0, a, b, o0, o1, reads, writes):
        if o1 is None:
            op("v", lambda: g.vector.tensor_scalar(out, in0, a, None, o0), reads, writes)
        else:
            op("v", lambda: g.vector.tensor_scalar(out, in0, a, b, o0, o1), reads, writes)

    def tt(out, a, b, o, reads, writes):
        op("v", lambda: g.vector.tensor_tensor(out, a, b, o), reads, writes)

    def cp(out, a, reads, writes):
        op("v", lambda: g.vector.tensor_copy(out, a), reads, writes)

    def fill(ap, val, writes):
        op("v", lambda: g.vector.memset(ap, val), [], writes)

    def act(out, in_, func, reads, writes, bias=0.0, scale=1.0):
        op("s", lambda: g.scalar.activation(out, in_, func, bias=bias, scale=scale), reads, writes)

    def iota(out, pattern, base, ch, writes):
        op("g", lambda: g.iota(out, pattern, base, ch, allow_small_or_imprecise_dtypes=True), [], writes)

    def blk(name, k, m=1):
        return T[name][:, 48 * k:48 * (k + m)]

    def ks(name, r):
        return ["%s%d" % (name, k) for k in r]

    dma("y", T.STI[:], T.st[:], "dSt", 16, [], ["STI"])
    dma("s", T.J0[:, 0:1024], T.jm[:, 0:1024], "dJA", 16, [], ["J0a"])
    dma("y", T.Y0W[:, 0:48], T.y0[:], "dLo", 48, [], ["Y0W"])
    for d in range(1, n):
        s = (rank - d) % n
        for l in range(2):
            a = (s * 2 + l) * 768
            dma("s", T.LTD[2 * s + l], T.lt[:, a:a + 768], "dLr", 96, [], ["LTS"])
    for l in range(2):
        a = (rank * 2 + l) * 768
        dma("y", T.LTA[:, 48 * l:48 * l + 48], T.lt[:, a:a + 768], "dLo", 48, [], ["LTA0"])
    dma("y", T.J0[:, 1024:2048], T.jm[:, 1024:2048], "dJB", 16, [], ["J0b"])
    dma("s", T.C0[:, 0:2048], T.cf[:], "dC", 16, [], ["C0"])
    for d in range(1, n):
        for a, w, k in (("aJ", "J", 32), ("aC", "C", 32), ("aL", "LTA", 8 if d != 2 else 2)):
            nm = "%s%d" % (a, d)
            lastw["%s%d" % (w, d)] = (nm, k, {nm: k})

    iota(T.PI[:, 0:1], [[0, 1]], 0, 1, ["PI"])
    iota(T.V8[:], [[-16, 8]], 0, 1, ["V8"])
    iota(T.IOT[:, 0:512], [[1, 512]], 0, 0, ["IOT0"])
    iota(T.XR[:], [[1, 32]], 0, 0, ["XR"])
    iota(T.JR[:], [[16, 48]], 0, 0, ["JR"])
    iota(T.IV[:], [[-1, 128]], 0, 1, ["IV"])

    for d in range(4):
        fill(T["J%d" % d][:, 2048:2056], 0, ["Jz%d" % d])
        fill(T["C%d" % d][:, 2048:2064], 0.0, ["Cz%d" % d])
    fill(T.SBB[:], 0.0, ["SBB"])
    fill(T.ONE[:], 1.0, ["ONE"])
    ts(T.PJ[:, 0:1], T.PI[:, 0:1], 15, None, A.bitwise_and, None, ["PI"], ["PJ"])
    ts(T.V8A[:], T.V8[:], -0.5, None, A.is_gt, None, ["V8"], ["V8A"])
    ts(T.V8B[:], T.V8[:], 15.5, None, A.is_lt, None, ["V8"], ["V8B"])
    cp(T.PC[:, 0:1], T.PJ[:, 0:1], ["PJ"], ["PC"])
    tt(T.SBB[:, 15:143:16], T.V8A[:], T.V8B[:], A.mult, ["V8A", "V8B"], ["SBB"])
    for k in (1, 2, 3):
        ts(T.IOT[:, 512 * k:512 * k + 512], T.IOT[:, 0:512], 512.0 * k, None, A.add, None, ["IOT0"], ["IOT%d" % k])
    cp(T.SBF[:], T.SBB[:], ["SBB"], ["SBF"])
    ts(T.ET[:], T.XR[:], T.PC[:, 0:1], None, A.is_equal, None, ["XR", "PC"], ["ET"])
    ts(T.IDF[:], T.IV[:], 0.0, None, A.is_equal, None, ["IV"], ["IDF"])

    def sels(o, buf, rd, sb="SBF", contiguous=False):
        src = T[buf]
        out = []
        for h in range(16):
            v = src[:, 48 * h:48 * h + 48] if contiguous else src[:, h:768:16]
            out.append((o, T[sb][:, 15 - h:143 - h], v, [rd, sb]))
        return out

    def starts(t):
        op("v", lambda: g.vector.tensor_copy(T.STF[:], T.IOT[:, 0:2048].indirect(blk("STU", t))), ks("IOT", range(4)) + ["STU"], ["STF"])
        pe(sels(T.KEY[:, 512 * t:512 * t + 48], "STF", "STF", contiguous=True), ["KEY%d" % t])

    def starts2(t):
        ts(blk("OFS", t), T.KEY[:, 512 * t:512 * t + 48], 0.0625, None, A.mult, None, ["KEY%d" % t], ["OFS%d" % t])

    def letters(d):
        src, k = T.LTA[:, 96 * d:96 * d + 96], 2 * d + 1
        L = "LTA%d" % d
        cp(T.LU[:, 96 * d:96 * d + 96], src, [L], ["LU%d" % d])
        ts(blk("Z0", k, 2), src, 15.5, 4096.0, A.is_gt, A.mult, [L], ks("Z0_", (k, k + 1)))
        ts(blk("Z02", k, 2), src, 15.5, 8192.0, A.is_gt, A.mult, [L], ks("Z02_", (k, k + 1)))
        if d == 0:
            tt(blk("ZZ0", 1), blk("Z02", 1), blk("Z0", 2), A.subtract, ["Z02_1", "Z0_2"], ["ZZ0_1"])
        else:
            e = 2 * d
            tt(blk("ZZ0", e, 2), blk("Z02", e, 2), blk("Z0", e + 1, 2), A.subtract,
               ks("Z02_", (e, e + 1)) + ks("Z0_", (e + 1, e + 2)), ks("ZZ0_", (e, e + 1)))
        if d == 3:
            cp(blk("ZZ0", 8), blk("Z02", 8), ["Z02_8"], ["ZZ0_8"])

    def onehot(k):
        off = T.Y0U[:] if k == 0 else T.LU[:, 48 * (k - 1):48 * k]
        act(T["OH%d" % k][:], T.ET[:].indirect(off), F.Copy, ["ET", "Y0U" if k == 0 else "LU%d" % ((k - 1) // 2)], ["OH%d" % k])

    lo = [0]

    def fused(items, reads):
        need("g", deps("g", reads, []))
        tr = []
        for c, e, i, o, s in items:
            rid, pid = topo.addr(c, core)
            tr.append(RemoteDMATransfer(dst_ids=[DstId(rid=rid, pnc=pid)], dma_engine_mask=sum(1 << b for b in e),
                                        remote_sem=T.sem[s], src=i, dst=o))
            lo[0] += len(e)
        g.remote_dma_fused(tr, local_sem=T.sem.lo)

    on = topo.engines(core, relays[0])
    direct = cores[(rank - 2) % n]
    off = topo.engines(core, direct)
    hi = [e for e in on if e not in off]

    def tabs(nm, i):
        return T[nm][:, 512 * i:512 * i + 512]

    def piece(c, e, d, out, a, sem):
        return [(c, e[l::2], T.LTD[2 * ((rank - d) % n) + l], T[out][:, a + 48 * l:a + 48 * l + 48], sem) for l in range(2)]

    def half(a, key):
        fused([(relays[a], on[0:8], tabs("J0", a), tabs("J0", a), "rJ"),
               (relays[a + 1], on[8:16], tabs("J0", a + 1), tabs("J0", a + 1), "rJ")], [key])

    half(0, "J0a")
    fused(piece(direct, off[0:2], 2, "LTA", 192, "aL2") + piece(relays[0], hi[0:4], 1, "LI1", 0, "rL") +
          piece(relays[2], hi[4:8], 3, "LI1", 0, "rL"), ["LTS"])
    half(2, "J0b")
    fused([(relays[i], on[4 * i:4 * i + 4], tabs("C0", i), tabs("C0", i), "rC") for i in range(4)], ["C0"])

    iota(T.D0S[:], [[0, 2304]], 0, 0, ["D0S"])
    iota(T.D0S[:, 0:2304:3], [[0, 768]], -1000, 0, ["D0S"])
    iota(T.D1S[:], [[0, 2304]], -255, 0, ["D1S"])
    iota(T.IR[0:1, :], [[0, 24], [-1, 16]], 15, 0, ["IR"])
    iota(T.PAT[:], [[0, 384]], 0, 0, ["PAT"])
    iota(T.PAT[:, 0:384:16], [[0, 24]], -16384, 0, ["PAT"])
    iota(T.EBA[0:48, :], [[0, 768]], 1, 0, ["EBA"])
    op("g", lambda: g.affine_select(T.EBB[0:48, :], T.EBA[0:48, :], [[1, 768]], A.is_ge, 0.0, 0, -16), ["EBA"], ["EBB"])
    op("g", lambda: g.affine_select(T.EBC[0:48, :], T.EBB[0:48, :], [[-1, 768]], A.is_ge, 0.0, 15, 16), ["EBB"], ["EBC"])

    def holes(nm, zeros):
        fill(T[nm][:, 0:3840:5], -1000.0, [nm + "c0"])
        for i in zeros:
            fill(T[nm][:, i:3840:5], 0.0, [nm + "c%d" % i])

    D1K = ["D1_0", "D1_1"]
    fill(T.D1[:], -255.0, D1K)
    cp(T.STU[:], T.STI[:], ["STI"], ["STU"])
    starts(0)
    holes("D0A", (1, 2, 4))
    cp(T.Y0U[:], T.Y0W[:, 0:48], ["Y0W"], ["Y0U"])
    onehot(0)
    letters(0)
    onehot(1)
    onehot(2)
    starts2(0)
    ts(T.JW[:], T.JR[:], T.PC[:, 0:1], None, A.add, None, ["JR", "PC"], ["JW"])
    ts(T.P15[:, 0:1], T.PC[:, 0:1], -1.0, 15.0, A.mult, A.add, ["PC"], ["P15"])
    ts(T.B5[:], T.JW[:], 5.0, BIG, A.mult, A.add, ["JW"], ["B5"])
    ts(T.DD[:], T.JW[:], 3.0, 15362.0, A.mult, A.add, ["JW"], ["DD"])
    ts(T.IDB[:], T.IV[:], 0.0, None, A.is_equal, None, ["IV"], ["IDB"])
    ts(T.ID16[:], T.IV[:], 0.0, 16.0, A.is_equal, A.mult, ["IV"], ["ID16"])
    ts(T.SBX[:], T.SBB[:], T.PC[:, 0:1], None, A.mult, None, ["SBB", "PC"], ["SBX"])

    XP = ["XA", "XB"]
    KP = ["KA", "KBK"]

    def jkeys(d):
        return ["J0a", "J0b", "Jz0"] if d == 0 else ["J%d" % d, "Jz%d" % d]

    def walk(t, gaps):
        slots = list(range(1 - t, 9))
        first = slots[0]
        ZN, ZZN = "Z%d" % t, "ZZ%d" % t
        MK = "M%d" % t
        M = T[MK]

        def zk(k):
            return "%s_%d" % (ZN, k)

        def step_j(k):
            if k < first:
                d, offs, oh, rd = 0, blk("OFS", t), (T.OH0 if t == 0 else T.OHY), ["OFS%d" % t, "OH0" if t == 0 else "OHY"]
            else:
                d, offs, oh, rd = (k - 1) // 2 if k else 0, T.OFJ[:], T["OH%d" % k], ["OFJ", "OH%d" % k]
            m = "MJ%d" % (k % 2)
            tt(T[m][:], T["J%d" % d][:, 0:2056].indirect(offs), oh[:], A.mult, rd + jkeys(d), [m])

        def step_x(k):
            X = XP[k % 2]
            o = T[X][:, 0:48]
            m = "MJ%d" % (k % 2)
            items = [(o, T.IDF[:], blk(ZN, k + 1), ["IDF", zk(k + 1)])] if k < 8 else []
            items += sels(o, m, m)
            if k >= first:
                b = "BE%d" % (k % 2)
                items.append((o, T.IDF[:], T[b][:], ["IDF", b]))
            pe(items, [X])

        def step_off(k):
            X = XP[k % 2]
            if k < 8:
                b = "BE%d" % ((k + 1) % 2)
                ts(T.OFJ[:], T[X][:, 0:48], 2048.0, None, A.min, None, [X], ["OFJ"])
                step_c1(k)
                ts(T[b][:], T[X][:, 0:48], -4096.0, 0.0, A.add, A.max, [X], [b])
            else:
                step_c1(k)

        def step_c1(k):
            X, a = XP[k % 2], "TC%d" % (k % 2)
            if k < first:
                tt(T[a][:], T[X][:, 0:48], blk(ZN, first), A.subtract, [X, zk(first)], [a])
            else:
                tt(T[a][:], T[X][:, 0:48], blk(ZZN, k), A.add, [X, "%s_%d" % (ZZN, k)], [a])

        def step_c(k):
            a, o = "TC%d" % (k % 2), "OC%d" % (k % 2)
            ts(T[o][:], T[a][:], 2048.0, None, A.min, None, [a], [o])
            d = (k - 1) // 2 if k >= max(first, 1) else 0
            win = T["C%d" % d][:, 0:2056].indirect(T[o][:])
            rd = ["C%d" % d, "Cz%d" % d, o]
            if k < first:
                act(T.D1[:, 0:3840:5], win, F.Copy, rd, D1K, scale=-1.0)
            elif k == 8:
                act(T.D0S[:, 1:2304:3], win, F.Copy, rd, ["D0S"])
            else:
                b = "D0A" if (k // 2) % 2 == 0 else "D0B"
                act(T[b][:, 1 + 2 * (k % 2):3840:5], win, F.Copy, rd, [b])

        def scan(gr, hf):
            if gr == 4:
                a, w, x, y, dk = 1152 * hf, 1152, T.D0S, T.D1S, ["D0S", "D1S"]
            else:
                nm = ("D0A", "D0B")[gr % 2]
                a, w, x, y = 1920 * hf, 1920, T[nm], T.D1
                dk = [nm + e for e in ("", "c0", "c2", "c4") + (() if gr % 2 else ("c1",))] + ["D1_%d" % hf]
            b = 3840 * gr + a
            op("v", lambda: g.vector.tensor_tensor_scan(T.OUT[:, b:b + w], x[:, a:a + w], y[:, a:a + w], 0.0, A.subtract, A.max),
               dk, ["OUT%d_%d" % (gr, hf)])

        def carry(gr, hf, q):
            a = 3840 * (gr - 1) + 1920 * hf
            src = T.OUT[:, a + 4:a + 1920:5]
            if gr == 4:
                out, w = T.D1S[:, 1152 * hf:1152 * hf + 1152:3], ["D1S"]
            else:
                out, w = T.D1[:, 1920 * hf:1920 * hf + 1920:5], ["D1_%d" % hf]
            rd = ["OUT%d_%d" % (gr - 1, hf)]
            if q == "v":
                cp(out, src, rd, w)
            else:
                act(out, src, F.Copy, rd, w)

        how = {}

        def sign(k, q, hf):
            if k < first:
                return
            gr, a = k // 2, 768 * (k % 2) + 384 * hf
            if k == 8:
                src = T.OUT[:, 15362 + 1152 * hf:15360 + 1152 * hf + 1152:3]
            else:
                b = 3840 * gr + 1920 * hf
                src = T.OUT[:, b + 2 + 2 * (k % 2):b + 1920:5]
            rd, o = ["OUT%d_%d" % (gr, hf)], T["SG%d" % (gr % 2)][:, a:a + 384]
            w = ["SG%d_%d%d" % (gr % 2, k % 2, hf)]
            how[k] = q
            if q == "v":
                ts(o, src, 0.0, -1.0, A.is_gt, A.mult, rd, w)
            else:
                act(o, src, F.Sign, rd, w, bias=0.5, scale=-1.0)

        def count(gr):
            k0, k1 = max(2 * gr, first), min(2 * gr + 1, 8)
            m, p, a = k1 - k0 + 1, gr % 2, 768 * (k0 % 2)
            o = T[KP[p]][:, 0:48 * m]
            rd = ["SG%d_%d%d" % (p, k % 2, hf) for k in range(k0, k1 + 1) for hf in (0, 1)] + ["SBB"]
            pe([(o, T.IDF[:], blk(ZN, k0, m), ["IDF"] + [zk(k) for k in range(k0, k1 + 1)])] +
               [(o, T.SBB[:, 15 - h:143 - h], T["SG%d" % p][:, a + h:a + 768 * m:16], rd) for h in range(16)], [KP[p]])

        def judge1(gr):
            p = KP[gr % 2]
            k0, k1 = max(2 * gr, first), min(2 * gr + 1, 8)
            for k in range(k0, k1 + 1):
                out, w = (M, MK) if k == first else (T.EE, "EE") if k % 2 == 0 else (T.EF, "EF")
                thr = -8.5 if how[k] == "v" else -1.0
                ts(out[:], T[p][:, 48 * (k - k0):48 * (k - k0) + 48], thr, QK[k], A.is_lt, A.mult, [p], [w])

        def judge2(gr):
            for k in range(max(2 * gr, first + 1), min(2 * gr + 1, 8) + 1):
                w = "EE" if k % 2 == 0 else "EF"
                tt(M[:], M[:], T[w][:], A.max, [MK, w], [MK])

        def leave(kk):
            if t == 0:
                return
            for k in kk:
                ts(blk("LD", k), M[:], QK[k], 16.0, A.is_equal, A.mult, [MK], ["LD%d" % k])
            if kk[0]:
                a, m = kk[0] - 1, len(kk)
                tt(blk("LF", a, m), blk("LT1", a, m), blk("LD", a + 1, m), A.max, ["LT1"] + ks("LD", kk), ks("LF", kk))
                return
            ts(T.DM[:], T.M0[:], 0.5, 16.0, A.is_gt, A.mult, ["M0"], ["DM"])
            tt(T.DL[:], blk("LD", 0), T.DM[:], A.max, ["LD0", "DM"], ["DL"])
            tt(T.YI0[:, 0:48], T.Y0W[:, 0:48], T.DL[:], A.max, ["Y0W", "DL"], ["YI0"])

        def goes(d):
            rd, src = ks("LF", (2 * d + 1, 2 * d + 2)), T.LF[:, 96 * d:96 * d + 96]
            if d == 2:
                fused([(cores[(rank + 2) % n], off[0:2], src, T.LI2[:], "aF2")], rd)
            else:
                fused([(relays[0 if d == 3 else 2], hi[0:8], src, T.LI2[:], "rF")], rd)

        step_j(first - 1)
        step_x(first - 1)
        for f in gaps.get(first - 1, []):
            f()
        step_off(first - 1)
        step_c(first - 1)
        late = []
        for k in slots:
            step_j(k)
            for f in late:
                f()
            late = []
            step_x(k)
            gr, hf = (k - 2) // 2, k % 2
            due = {5: 0, 7: 1}.get(k)
            if due is not None:
                judge1(due)
            if k >= 2:
                scan(gr, hf)
                if gr == 3 or t == 0:
                    carry(gr + 1, hf, "v")
                if gr < 3 and t == 0:
                    sign(2 * gr, "v", hf)
                    sign(2 * gr + 1, "s", hf)
            if due is not None:
                judge2(due)
            if k in (4, 6, 8):
                count((k - 4) // 2)
            for f in gaps.get(k, []):
                f()
            step_off(k)
            step_c(k)
            if t == 0 and k < 7:
                late.append(lambda k=k: onehot(k + 2))
            if k >= 2 and t == 1 and k < 8:
                late.append(lambda gr=gr, hf=hf: (carry(gr + 1, hf, "s"), sign(2 * gr, "s", hf), sign(2 * gr + 1, "s", hf)))
        scan(3, 1)
        carry(4, 1, "v")
        for hf in range(2):
            sign(6, "v", hf)
            sign(7, "s", hf)
        scan(4, 0)
        count(3)
        judge1(2)
        scan(4, 1)
        judge2(2)
        if t:
            sign(8, "v", 0)
            sign(8, "v", 1)
            count(4)
            leave((1, 2, 3, 4))
            goes(1)
        judge1(3)
        judge2(3)
        if t:
            judge1(4)
            judge2(4)
            leave((5, 6, 7, 8))
            goes(3)
        tt(T.T1[:], T.B5[:], M[:], A.subtract, ["B5", MK], ["T1"])
        tt(T.T2[:], T.T1[:], T.DD[:], A.min, ["T1", "DD"], ["T2"])
        cp(T.SEL[:], T.T2[:], ["T2"], ["SEL"])
        outs = ["OUT%d_%d" % (gr, hf) for gr in range(5) for hf in range(2)]
        for hf in range(2):
            ts(T.VF[:, 384 * hf:384 * hf + 384], T.OUT[:, 0:OUTW].indirect(T.SEL[:, 24 * hf:24 * hf + 24]), -1.0, None, A.mult, None,
               ["SEL"] + outs, ["VF%d" % hf])
            if hf == 0:
                if t == 0:
                    sign(8, "s", 0)
                    sign(8, "s", 1)
                    count(4)
                else:
                    goes(2)
                    leave((0,))
        return lambda: (judge1(4), judge2(4))

    fin = walk(0, {0: [lambda: holes("D0B", (2, 4))], 1: [lambda: letters(1), lambda: starts(1)], 2: [lambda: starts2(1)],
                   3: [lambda: letters(2)], 5: [lambda: letters(3)]})

    for hf in range(2):
        base = 512 * hf
        pe([(T.KEY[:, base:base + 384], T.ONE[0:1, :], T.IR[0:1, :], ["ONE", "IR"])] +
           [(T.KEY[:, base + 128 * b:base + 128 * b + 128], T.VF[:, 384 * hf + 128 * b:384 * hf + 128 * b + 128], T.ID16[:], ["VF%d" % hf, "ID16"])
            for b in range(3)], ["KEY%d" % hf])
    S8 = range(1, 9)
    for hf in range(2):
        op("v", lambda hf=hf: g.vector.tensor_tensor_scan(T.KM[:, 384 * hf:384 * hf + 384], T.PAT[:], T.KEY[:, 512 * hf:512 * hf + 384],
                                                         0.0, A.add, A.max), ["PAT", "KEY%d" % hf], ["KM%d" % hf])
    cp(T.KI[:], T.KM[:, 15:768:16], ["KM0", "KM1"], ["KI"])
    ts(T.KB[:], T.KI[:], 15, None, A.bitwise_and, None, ["KI"], ["KB"])
    cp(T.KC[:], T.KB[:], ["KB"], ["KC"])
    pe([(T.XA[0:48, 0:128], T.KC[:], T.IDB[:], ["KC", "IDB"])], ["XA"])
    cp(T.YT[0:48, :], T.XA[0:48, 0:128], ["XA"], ["YT"])
    for hf in range(2):
        for b in range(3):
            q = 3 * hf + b
            pe([(T.YB[:, 512 * hf + 128 * b:512 * hf + 128 * b + 128], T.EBC[0:48, 128 * q:128 * q + 128], T.YT[0:48, :], ["EBC", "YT"])],
               ["YB%d" % hf])
    fin()
    for k in S8:
        ts(blk("ZD", k), T.M0[:], QK[k], 4096.0, A.is_equal, A.mult, ["M0"], ["ZD%d" % k])
    ts(blk("Z1", 0), T.M0[:], 0.5, 4096.0, A.is_gt, A.mult, ["M0"], ["Z1_0"])
    Z1K = ks("Z1_", range(9))
    for hf in range(2):
        ts(T.OHY[:, 384 * hf:384 * hf + 384], T.YB[:, 512 * hf:512 * hf + 384], T.P15[:, 0:1], None, A.is_equal, None,
           ["YB%d" % hf, "P15"], ["OHY"])

    def marks():
        tt(blk("Z1", 1, 8), blk("Z0", 1, 8), blk("ZD", 1, 8), A.add, ks("ZD", S8) + ks("Z0_", S8), Z1K[1:])
        ts(T.Z12[:], T.Z1[:], 2.0, None, A.mult, None, Z1K, ["Z12"])

    def marks2():
        tt(blk("ZZ1", 0, 8), blk("Z12", 0, 8), blk("Z1", 1, 8), A.subtract, ["Z12"] + Z1K, ks("ZZ1_", range(8)))
        cp(blk("ZZ1", 8), blk("Z12", 8), ["Z12"], ["ZZ1_8"])

    def kept():
        ts(T.LZ[:], blk("Z1", 1, 8), 1.0 / 256.0, None, A.mult, None, Z1K, ["LZ"])
        tt(T.LT1[:], T.LTA[:], T.LZ[:], A.max, ["LZ"] + ks("LTA", range(4)), ["LT1"])

    def newword():
        pe(sels(T.YB[:, 0:48], "OHY", "OHY", "SBX"), ["YB0"])

    def newword2():
        cp(T.Y1W[:], T.YB[:, 0:48], ["YB0"], ["Y1W"])

    walk(1, {-1: [marks], 0: [marks2], 1: [kept, newword], 2: [newword2]})

    ts(T.DM[:], T.M1[:], 0.5, 16.0, A.is_gt, A.mult, ["M1"], ["DM"])
    tt(T.YI1[:, 0:48], T.Y1W[:], T.DM[:], A.max, ["Y1W", "DM"], ["YI1"])
    for h in range(16):
        out, src = T.VN[:, 48 * h:48 * h + 48], T.VF[:, h:768:16]
        if h % 2:
            act(out, src, F.Copy, ["VF0", "VF1"], ["VN%d" % h])
        else:
            cp(out, src, ["VF0", "VF1"], ["VN%d" % h])
    total = 16 * 11
    dma("y", T.yi[:, 0:768], T.YI0[:, 0:48], "dO", total, ["YI0"], ["o1"])
    for l in range(2):
        a = (rank * 2 + l) * 768
        dma("y", T.yl[:, a:a + 768], T.LF[:, 48 * l:48 * l + 48], "dO", total, ["LF%d" % (l + 1)], ["o2%d" % l])

    def home(d):
        s = (rank - d) % n
        nm = "aF%d" % d
        k = 2 if d == 2 else 8
        lastw["LI%d" % d] = (nm, k, {nm: k})
        for l in range(2):
            a = (s * 2 + l) * 768
            dma("y", T.yl[:, a:a + 768], T["LI%d" % d][:, 48 * l:48 * l + 48], "dO", total, ["LI%d" % d], ["o3%d%d" % (d, l)])

    home(1)
    dma("y", T.yi[:, 768:1536], T.YI1[:, 0:48], "dO", total, ["YI1"], ["o4"])
    dma("y", T.yv[:], T.VN[:], "dO", total, ks("VN", range(16)), ["o5"])
    home(2)
    home(3)
    g.sync.wait_ge(T.sem.dO, total)
    for s, v in (("lo", lo[0]), ("qv", cnt["v"]), ("qs", cnt["s"]), ("qp", cnt["p"]), ("qg", cnt["g"]), ("dLr", 96)):
        g.wait_ge(T.sem[s], v)
